import numpy as np
import ml_dtypes


def mxq(x, axis, fmt="e4m3"):
    dtype, down = {"e4m3": (ml_dtypes.float8_e4m3fn, 7), "e5m2": (ml_dtypes.float8_e5m2, 14)}[fmt]
    v = np.moveaxis(np.asarray(x, np.float32).astype(ml_dtypes.bfloat16).astype(np.float64), axis, -1)
    blocks = v.reshape(v.shape[:-1] + (-1, 32))
    amax = np.abs(blocks).max(-1, keepdims=True)
    byte = np.maximum(np.where(amax > 0, np.frexp(amax)[1] - 1 + 127, 0) - down, 1)
    scale = np.exp2(byte - 127.0)
    codes = (blocks / scale).astype(np.float32).astype(dtype).astype(np.float64)
    return np.moveaxis((codes * scale).reshape(v.shape), -1, axis)


WIDE = False


def mx_kscale(k):
    if not WIDE:
        return np.ones(k)
    levels = np.array([10, -10, 5, -5, 0])
    if k % 512:
        return np.exp2(np.random.permutation(np.resize(levels, k // 32))).repeat(32)
    a = np.empty((k // 512, 16))
    for p in range(k // 512):
        a[p, :8] = np.random.permutation(np.resize(levels, 8))
        for g in range(8):
            far = levels[np.abs(levels - a[p, g]) >= 10]
            a[p, g + 8] = far[np.random.randint(len(far))]
    return np.exp2(a.ravel()).repeat(32)


BF16 = ml_dtypes.bfloat16


def bf(x):
    return np.asarray(x, np.float32).astype(BF16)


def f64(x):
    return np.asarray(x).astype(np.float64)


E2M1 = np.array([0.0, 0.5, 1.0, 1.5, 2.0, 3.0, 4.0, 6.0, -0.0, -0.5, -1.0, -1.5, -2.0, -3.0, -4.0, -6.0])


def pack_weight(w, fmt):
    k, n = w.shape
    w = f64(bf(w)).reshape(k // 32, 32, n)
    amax = np.abs(w).max(1)
    if fmt == "e4m3":
        byte = np.frexp(amax)[1] - 1 + 127 - 7
    else:
        mant, ex = np.frexp(amax / 6.0)
        byte = np.where(mant > 0.5, ex, ex - 1) + 127
    byte = np.clip(np.where(amax > 0, byte, 1), 1, 254)
    scaled = (w * np.exp2(127.0 - byte)[:, None, :]).reshape(k, n).astype(np.float32)
    by_word = np.ascontiguousarray(scaled.reshape(k // 512, 128, 4, n).transpose(0, 1, 3, 2))
    if fmt == "e4m3":
        words = by_word.astype(ml_dtypes.float8_e4m3fn).view(np.uint8)
    else:
        c = by_word.astype(ml_dtypes.float4_e2m1fn).view(np.uint8) & 0xF
        words = c[..., 0::2] | (c[..., 1::2] << 4)
    return np.ascontiguousarray(words), np.ascontiguousarray(byte.astype(np.uint8).reshape(k // 512, 16, n))


def unpack_weight(words, scales, fmt):
    g, p, n, _ = words.shape
    if fmt == "e4m3":
        vals = np.ascontiguousarray(words).view(ml_dtypes.float8_e4m3fn).astype(np.float64)
    else:
        nib = np.empty((g, p, n, 4), np.uint8)
        nib[..., 0::2] = words & 0xF
        nib[..., 1::2] = words >> 4
        vals = E2M1[nib]
    vals = vals * np.repeat(np.exp2(scales.astype(np.float64) - 127.0), 8, axis=1)[..., None]
    return vals.transpose(0, 1, 3, 2).reshape(g * 512, n)
def pack4(w):
    words, scales = pack_weight(w, "e2m1")
    return words.reshape(words.shape[0], 128, -1), scales


def unpack4(words, scales):
    return unpack_weight(words.reshape(words.shape[0], 128, -1, 2), scales, "e2m1")


M, F, D, N, R = 1536, 2048, 1024, 512, 256


def draw0():
    s = mx_kscale(F)
    t = mx_kscale(D)
    u = mx_kscale(M)
    gate = np.random.standard_normal((M, F))
    up = np.random.standard_normal((M, F)) * s * u[:, None]
    w_down = np.random.standard_normal((F, D)) / np.sqrt(F) / s[:, None] * t
    resid = np.random.standard_normal((M, D)) * t * u[:, None]
    head_words, head_scales = pack4(np.random.standard_normal((D, N)) / np.sqrt(D) / t[:, None])
    pool = np.random.standard_normal((R, M)) / np.sqrt(M) / u
    return {"gate": bf(gate), "up": bf(up), "w_down": bf(w_down), "resid": bf(resid),
            "head_words": head_words, "head_scales": head_scales, "pool": bf(pool)}


def core(gate, up, w_down, resid, head_words, head_scales, pool):
    h = np.maximum(f64(gate), 0.0) * f64(up)
    z = (mxq(h, 1, "e4m3") @ mxq(f64(w_down), 0, "e4m3")) + f64(resid)
    y = mxq(z, 1, "e4m3") @ unpack4(head_words, head_scales)
    c = mxq(f64(pool), 1, "e4m3") @ mxq(z, 0, "e4m3")
    return y, c


def e4m3fn_bytes(y):
    return np.clip(np.asarray(y, np.float64), -448.0, 448.0).astype(np.float32).astype(ml_dtypes.float8_e4m3fn).view(np.uint8)


def e4m3fn_values(b):
    return np.asarray(b, np.uint8).view(ml_dtypes.float8_e4m3fn).astype(np.float64)


def setup_inputs():
    d = draw0()
    x0 = np.asarray(d['pool']).astype(np.float64)
    s = (np.max(np.abs(x0), axis=(0,), keepdims=True) / 448.0).astype(np.float32)
    out = {}
    for k, v in d.items():
        if k == 'pool':
            out['pool_bytes'] = e4m3fn_bytes(x0 / s.astype(np.float64))
            out['pool_scale'] = s
        else:
            out[k] = v
    return out


def reference(gate, up, w_down, resid, head_words, head_scales, pool_bytes, pool_scale):
    return core(gate, up, w_down, resid, head_words, head_scales, e4m3fn_values(pool_bytes) * pool_scale.astype(np.float64))

@@ -1,0 +1,472 @@
+from contextlib import ExitStack
+
+import concourse.mybir as mybir
+from concourse.masks import make_identity
+
+M, F, D, N, R = 1536, 2048, 1024, 512, 256
+FLOPS = 2 * M * F * D + 2 * M * D * N + 2 * R * M * D
+
+F32 = mybir.dt.float32
+BF16 = mybir.dt.bfloat16
+I32 = mybir.dt.int32
+U32 = mybir.dt.uint32
+U8 = mybir.dt.uint8
+FP8 = mybir.dt.float8_e4m3fn
+FP8X4 = mybir.dt.float8_e4m3fn_x4
+FP4X4 = mybir.dt.float4_e2m1fn_x4
+ADD = mybir.AluOpType.add
+MULT = mybir.AluOpType.mult
+RELU = mybir.ActivationFunctionType.Relu
+
+P = 128
+PACK = 4
+K_PASS = P * PACK
+TILES = M // P
+GROUPS = M // K_PASS
+F_PASSES = F // K_PASS
+HALF = 512
+HALVES = D // HALF
+CHUNK = HALF // 2
+SLOT_TILES = R // P
+
+W_SPLIT = HALF // 2
+ALL = slice(0, F)
+LEFT, RIGHT = slice(0, F // 2), slice(F // 2, F)
+RELU_VECTOR, RELU_SCALAR = slice(0, 7 * F // 8), slice(7 * F // 8, F)
+RUN = 4
+
+
+def tile_reglu_down_two_reads_s8_kernel(
+    tc, gate, up, w_down, resid, head_words, head_scales, pool_bytes, pool_scale, out_y, out_c
+):
+    nc = tc.nc
+
+    gate_v = gate.rearrange("(g p t) f -> g p t f", p=P, t=PACK)
+    up_v = up.rearrange("(g p t) f -> g p t f", p=P, t=PACK)
+    resid_v = resid.rearrange("(g p t) d -> g p t d", p=P, t=PACK)
+    y_v = out_y.rearrange("(g p t) n -> g p t n", p=P, t=PACK)
+    w_v = w_down.rearrange("(g p j) d -> g p j d", p=P, j=PACK)
+
+    with ExitStack() as ctx:
+        keep = ctx.enter_context(tc.tile_pool(name="keep", bufs=1))
+        sb = ctx.enter_context(tc.tile_pool(name="sb", bufs=2))
+        psum = ctx.enter_context(tc.psum_pool(name="psum", bufs=2))
+
+        w_codes = keep.tile([P, F_PASSES, D], U32, name="w_codes", align_bytes=64)
+        w_scales = keep.tile([P, F_PASSES, D], U8, name="w_scales", align_bytes=64)
+        z_codes = keep.tile([P, GROUPS, D], U32, name="z_codes", align_bytes=64)
+        z_scales = keep.tile([P, GROUPS, D], U8, name="z_scales", align_bytes=64)
+        pool_codes = keep.tile([P, GROUPS, R], U32, name="pool_codes", align_bytes=64)
+        pool_scales = keep.tile([P, GROUPS, R], U8, name="pool_scales", align_bytes=64)
+        head_sb = keep.tile([P, HALVES, 2 * N], U8, name="head_sb", align_bytes=64)
+        head_sc = keep.tile([P, HALVES, N], U8, name="head_sc", align_bytes=64)
+        code_bytes = keep.tile([P, SLOT_TILES, M], U8, name="code_bytes", align_bytes=64)
+        scale_row = keep.tile([P, M], F32, name="scale_row", align_bytes=64)
+        pool_bf = keep.tile([P, SLOT_TILES, M], BF16, name="pool_bf", align_bytes=64)
+        ident = keep.tile([P, P], F32, name="ident", align_bytes=64)
+
+        gates, ups, resids, relus, hs, hbanks, hts, hcs, hss = {}, {}, {}, {}, {}, {}, {}, {}, {}
+        accs, zs, zbanks, zts, zcs, zss, ybanks = {}, {}, {}, {}, {}, {}, {}
+        wraws, wgs, zis, pbanks, pts, cbanks = {}, {}, {}, {}, {}, {}
+
+
+        def load_gate(i, cols=ALL):
+            if i < TILES:
+                if i not in gates:
+                    gates[i] = sb.tile([P, F], BF16, tag="gate", name="gate_sb", bufs=4, align_bytes=64)
+                nc.sync.dma_start(out=gates[i][:, cols], in_=gate_v[i // PACK][:, i % PACK, cols])
+
+        def load_up(i, cols=ALL):
+            if i < TILES:
+                if i not in ups:
+                    ups[i] = sb.tile([P, F], BF16, tag="up", name="up_sb", bufs=4, align_bytes=64)
+                nc.sync.dma_start(out=ups[i][:, cols], in_=up_v[i // PACK][:, i % PACK, cols])
+
+        def load_resid(i):
+            if i < TILES:
+                resids[i] = sb.tile([P, D], BF16, tag="resid", name="resid_sb", bufs=4, align_bytes=64)
+                nc.sync.dma_start(out=resids[i][:], in_=resid_v[i // PACK][:, i % PACK, :])
+
+        def load_w(g, h):
+            wraws[g, h] = sb.tile([P, PACK, HALF], BF16, tag="wraw", name="w_raw", bufs=8, align_bytes=64)
+            nc.sync.dma_start(out=wraws[g, h][:], in_=w_v[g][:, :, h * HALF : (h + 1) * HALF])
+
+        def load_head():
+            nc.sync.dma_start(out=head_sb[:], in_=head_words.rearrange("g p b -> p g b"))
+
+        def load_head_scales():
+            for q in range(PACK):
+                rows = slice(32 * q, 32 * q + 4)
+                nc.sync.dma_start(
+                    out=head_sc[rows, :, :].bitcast(I32),
+                    in_=head_scales[:, 4 * q : 4 * q + 4, :].rearrange("g q n -> q g n").bitcast(I32),
+                )
+
+        def load_pool():
+            nc.sync.dma_start(out=scale_row[:], in_=pool_scale.rearrange("o k -> (o k)").partition_broadcast(P))
+            nc.sync.dma_start(out=code_bytes[:], in_=pool_bytes.rearrange("(a p) m -> p a m", p=P))
+
+
+        def group_w(g, h):
+            wgs[g, h] = sb.tile([P, HALF, PACK], BF16, tag="wg", name="w_grouped", bufs=3, align_bytes=64)
+            for copy, cols in ((nc.scalar.copy, slice(0, W_SPLIT)), (nc.vector.tensor_copy, slice(W_SPLIT, HALF))):
+                copy(
+                    out=wgs[g, h][:, cols, :].rearrange("p (c i) j -> p c j i", i=RUN),
+                    in_=wraws[g, h][:, :, cols].rearrange("p j (c i) -> p c j i", i=RUN),
+                )
+
+        def quant_w(g, h):
+            cols = slice(h * HALF, (h + 1) * HALF)
+            nc.vector.quantize_mx(
+                out=w_codes[:, g, cols].bitcast(FP8X4),
+                scales=w_scales[:, g, cols],
+                in_=wgs[g, h][:].rearrange("p w j -> p (w j)"),
+            )
+
+
+        def relu_tile(i):
+            if i not in relus:
+                relus[i] = sb.tile([P, F], BF16, tag="relu", name="relu_sb", bufs=2, align_bytes=64)
+            return relus[i]
+
+        def relu_v(i, cols):
+            if i < TILES:
+                nc.vector.tensor_scalar_max(relu_tile(i)[:, cols], gates[i][:, cols], 0.0)
+
+        def relu_s(i, cols):
+            if i < TILES:
+                nc.scalar.activation(relu_tile(i)[:, cols], gates[i][:, cols], func=RELU)
+
+        def product(i, cols=ALL):
+            if i < TILES:
+                if i not in hs:
+                    hs[i] = sb.tile([P, F], BF16, tag="h", name="h_sb", bufs=2, align_bytes=64)
+                quads = slice(cols.start // 4, cols.stop // 4)
+                nc.vector.tensor_tensor(
+                    out=hs[i][:].rearrange("p (u q e) -> p u q e", u=2, e=2)[:, :, quads, :],
+                    in0=relus[i][:, cols].rearrange("p (q u e) -> p u q e", u=2, e=2),
+                    in1=ups[i][:, cols].rearrange("p (q u e) -> p u q e", u=2, e=2),
+                    op=MULT,
+                )
+
+        def turn_h(i):
+            words = hs[i][:].bitcast(F32)
+            for b in range(2):
+                hbanks[i, b] = psum.tile([P, 2, 2, P], F32, tag="turned", name="h_turned", bufs=2)
+                for gb in range(2):
+                    for u in range(2):
+                        w0 = u * (F // 4) + (2 * b + gb) * P
+                        nc.tensor.transpose(hbanks[i, b][:, gb, u, :], words[:, w0 : w0 + P], ident[:])
+
+        def empty_h(i, b):
+            if i not in hts:
+                hts[i] = sb.tile([P, F_PASSES, P, 2], F32, tag="ht", name="h_grouped", bufs=2, align_bytes=64)
+            nc.scalar.copy(
+                out=hts[i][:, 2 * b : 2 * b + 2, :, :], in_=hbanks[i, b][:].rearrange("p g u m -> p g m u")
+            )
+
+        def quant_h(i):
+            hcs[i] = sb.tile([P, F_PASSES * P], U32, tag="hc", name="h_codes", bufs=2, align_bytes=64)
+            hss[i] = sb.tile([P, F_PASSES * P], U8, tag="hs", name="h_scales", bufs=2, align_bytes=64)
+            nc.vector.quantize_mx(
+                out=hcs[i][:].bitcast(FP8X4),
+                scales=hss[i][:],
+                in_=hts[i][:].rearrange("p g m u -> p (g m u)").bitcast(BF16),
+            )
+
+
+        def down(i, h):
+            accs[i, h] = psum.tile([P, HALF], F32, tag="acc", name="z_acc", bufs=4)
+            cols = slice(h * HALF, (h + 1) * HALF)
+            for g in range(F_PASSES):
+                toks = slice(g * P, (g + 1) * P)
+                nc.tensor.matmul_mx(
+                    out=accs[i, h][:],
+                    lhsT=hcs[i][:, toks].bitcast(FP8X4),
+                    lhsT_scale=hss[i][:, toks],
+                    rhs=w_codes[:, g, cols].bitcast(FP8X4),
+                    rhs_scale=w_scales[:, g, cols],
+                    start=(g == 0),
+                    stop=(g == F_PASSES - 1),
+                )
+
+        def add_resid(i, h):
+            G, t = divmod(i, PACK)
+            if G not in zs:
+                zs[G] = sb.tile([P, PACK, D], BF16, tag="z", name="z_sb", bufs=2, align_bytes=64)
+            cols = slice(h * HALF, (h + 1) * HALF)
+            nc.vector.tensor_tensor(
+                out=zs[G][:, t, cols].rearrange("p (u q e) -> p u q e", u=2, e=2),
+                in0=accs[i, h][:].rearrange("p (q u e) -> p u q e", u=2, e=2),
+                in1=resids[i][:, cols].rearrange("p (q u e) -> p u q e", u=2, e=2),
+                op=ADD,
+            )
+
+
+        def turn_z(i):
+            G, t = divmod(i, PACK)
+            words = zs[G][:, t, :].bitcast(F32)
+            zbanks[i] = psum.tile([P, HALVES, 2, P], F32, tag="mixed", name="z_turned", bufs=2)
+            for h in range(HALVES):
+                for u in range(2):
+                    w0 = h * (HALF // 2) + u * P
+                    nc.tensor.transpose(zbanks[i][:, h, u, :], words[:, w0 : w0 + P], ident[:])
+
+        def empty_z(i):
+            zts[i] = sb.tile([P, HALVES, P, 2], F32, tag="zt", name="zt_grouped", bufs=2, align_bytes=64)
+            nc.scalar.copy(out=zts[i][:], in_=zbanks[i][:].rearrange("p h u m -> p h m u"))
+
+        def quant_zt(i):
+            zcs[i] = sb.tile([P, HALVES * P], U32, tag="ztc", name="zt_codes", bufs=2, align_bytes=64)
+            zss[i] = sb.tile([P, HALVES * P], U8, tag="zts", name="zt_scales", bufs=2, align_bytes=64)
+            nc.vector.quantize_mx(
+                out=zcs[i][:].bitcast(FP8X4),
+                scales=zss[i][:],
+                in_=zts[i][:].rearrange("p h m u -> p (h m u)").bitcast(BF16),
+            )
+
+        def project(i):
+            ybanks[i] = psum.tile([P, N], F32, tag="mixed", name="y_acc", bufs=2)
+            for h in range(HALVES):
+                toks = slice(h * P, (h + 1) * P)
+                nc.tensor.matmul_mx(
+                    out=ybanks[i][:],
+                    lhsT=zcs[i][:, toks].bitcast(FP8X4),
+                    lhsT_scale=zss[i][:, toks],
+                    rhs=head_sb[:, h, :].bitcast(FP4X4),
+                    rhs_scale=head_sc[:, h, :],
+                    start=(h == 0),
+                    stop=(h == HALVES - 1),
+                )
+
+        def store_y(i):
+            y_sb = sb.tile([P, N], F32, tag="y", name="y_sb", bufs=3, align_bytes=64)
+            nc.scalar.copy(out=y_sb[:], in_=ybanks[i][:])
+            nc.sync.dma_start(out=y_v[i // PACK][:, i % PACK, :], in_=y_sb[:])
+
+
+        def group_z(copy, G, c, cols=slice(0, CHUNK)):
+            h, c0 = divmod(c * CHUNK, HALF)
+            if (G, h) not in zis:
+                zis[G, h] = sb.tile([P, HALF, PACK], BF16, tag="zi", name="z_grouped", bufs=2, align_bytes=64)
+            copy(
+                out=zis[G, h][:, c0 + cols.start : c0 + cols.stop, :].rearrange("p (c i) t -> p c t i", i=RUN),
+                in_=zs[G][:, :, c * CHUNK + cols.start : c * CHUNK + cols.stop].rearrange(
+                    "p t (c i) -> p c t i", i=RUN
+                ),
+            )
+
+        def quant_z(G, h):
+            cols = slice(h * HALF, (h + 1) * HALF)
+            nc.vector.quantize_mx(
+                out=z_codes[:, G, cols].bitcast(FP8X4),
+                scales=z_scales[:, G, cols],
+                in_=zis[G, h][:].rearrange("p d t -> p (d t)"),
+            )
+
+        def scale_pool(a):
+            nc.vector.tensor_tensor(
+                out=pool_bf[:, a, :], in0=code_bytes[:, a, :].bitcast(FP8), in1=scale_row[:], op=MULT
+            )
+
+        def turn_pool(G, tag):
+            pbanks[G] = psum.tile([P, SLOT_TILES, 2, P], F32, tag=tag, name="pool_turned", bufs=2)
+            for a in range(SLOT_TILES):
+                words = pool_bf[:, a, G * K_PASS : (G + 1) * K_PASS].bitcast(F32)
+                for u in range(2):
+                    nc.tensor.transpose(pbanks[G][:, a, u, :], words[:, u : K_PASS // 2 : 2], ident[:])
+
+        def empty_pool(G):
+            pts[G] = sb.tile([P, SLOT_TILES, P, 2], F32, tag="zt", name="pool_grouped", bufs=2, align_bytes=64)
+            nc.scalar.copy(out=pts[G][:], in_=pbanks[G][:].rearrange("p a u r -> p a r u"))
+
+        def quant_pool(G):
+            nc.vector.quantize_mx(
+                out=pool_codes[:, G, :].bitcast(FP8X4),
+                scales=pool_scales[:, G, :],
+                in_=pts[G][:].rearrange("p a r u -> p (a r u)").bitcast(BF16),
+            )
+
+        def gather(h, groups):
+            cols = slice(h * HALF, (h + 1) * HALF)
+            for a in range(SLOT_TILES):
+                if (a, h) not in cbanks:
+                    tag, bufs = (("turned", 2), ("acc", 4))[h]
+                    cbanks[a, h] = psum.tile([P, HALF], F32, tag=tag, name="c_acc", bufs=bufs)
+                slots = slice(a * P, (a + 1) * P)
+                for G in groups:
+                    nc.tensor.matmul_mx(
+                        out=cbanks[a, h][:],
+                        lhsT=pool_codes[:, G, slots].bitcast(FP8X4),
+                        lhsT_scale=pool_scales[:, G, slots],
+                        rhs=z_codes[:, G, cols].bitcast(FP8X4),
+                        rhs_scale=z_scales[:, G, cols],
+                        start=(G == 0),
+                        stop=(G == GROUPS - 1),
+                    )
+
+        def store_c(copy, a, h):
+            c_sb = sb.tile([P, HALF], F32, tag="c", name="c_sb", bufs=4, align_bytes=64)
+            copy(
+                out=c_sb[:].rearrange("p (q u e) -> p q u e", u=2, e=2),
+                in_=cbanks[a, h][:].rearrange("p (u q e) -> p q u e", u=2, e=2),
+            )
+            nc.sync.dma_start(out=out_c[a * P : (a + 1) * P, h * HALF : (h + 1) * HALF], in_=c_sb[:])
+
+        with tc.manual_schedule():
+            load_w(0, 0)
+            load_w(1, 0)
+            load_gate(0, LEFT)
+            load_up(0, RIGHT)
+            load_gate(0, RIGHT)
+            load_w(2, 0)
+            load_up(0, LEFT)
+            load_w(3, 0)
+            load_w(0, 1)
+            load_gate(1)
+            load_w(1, 1)
+            load_up(1)
+            load_w(2, 1)
+            load_w(3, 1)
+            load_resid(0)
+            load_gate(2)
+            load_gate(3)
+            load_resid(1)
+            load_up(2)
+            load_head()
+            load_up(3)
+            nc.vector.memset(head_sc[:].rearrange("p g n -> p (g n)").bitcast(I32), 0)
+            make_identity(nc, ident[:])
+
+            group_w(0, 0)
+            group_w(1, 0)
+            relu_v(0, LEFT)
+            quant_w(0, 0)
+            relu_v(0, RIGHT)
+            quant_w(1, 0)
+            product(0, RIGHT)
+            group_w(2, 0)
+            product(0, LEFT)
+            turn_h(0)
+            quant_w(2, 0)
+            group_w(3, 0)
+            group_w(0, 1)
+            relu_v(1, ALL)
+            quant_w(3, 0)
+            quant_w(0, 1)
+            group_w(1, 1)
+            empty_h(0, 0)
+            empty_h(0, 1)
+            product(1)
+            turn_h(1)
+            group_w(2, 1)
+            quant_h(0)
+            load_gate(4)
+            load_head_scales()
+            load_resid(2)
+            load_up(4)
+            empty_h(1, 0)
+            down(0, 0)
+            quant_w(2, 1)
+            empty_h(1, 1)
+            quant_w(1, 1)
+            quant_h(1)
+            group_w(3, 1)
+            relu_v(2, ALL)
+            relu_s(3, ALL)
+            load_gate(5)
+            load_gate(6)
+            load_up(5)
+            quant_w(3, 1)
+            add_resid(0, 0)
+            product(2)
+            load_gate(7)
+            down(1, 0)
+            down(0, 1)
+            add_resid(0, 1)
+            load_up(6)
+            down(1, 1)
+            add_resid(1, 0)
+            add_resid(1, 1)
+
+            for s in range(1, TILES - 1):
+                product(s + 2)
+                if s == 3:
+                    store_y(0)
+                if s == TILES - 2:
+                    scale_pool(0)
+                turn_h(s + 1)
+                turn_z(s - 1)
+                load_resid(s + 2)
+                if s in (6, 8, 10):
+                    quant_z(*divmod((s - 6) // 2, HALVES))
+                empty_h(s + 1, 0)
+                empty_z(s - 1)
+                empty_h(s + 1, 1)
+                if s >= 3:
+                    store_y(s - 2)
+                if s == 2:
+                    project(0)
+                relu_v(s + 3, RELU_VECTOR)
+                quant_zt(s - 1)
+                if s >= 2:
+                    down(s, 0)
+                relu_s(s + 3, RELU_SCALAR)
+                if s >= 2:
+                    down(s, 1)
+                if s == 4:
+                    load_pool()
+                if s >= 2:
+                    project(s - 1)
+                    add_resid(s, 0)
+                quant_h(s + 1)
+                load_gate(s + 7)
+                load_up(s + 6)
+                if s >= 4:
+                    group_z(nc.scalar.copy, *divmod(s - 4, PACK))
+                if s >= 2:
+                    add_resid(s, 1)
+
+            last, G = TILES - 1, GROUPS - 1
+            group_z(nc.scalar.copy, G - 1, 3)
+            scale_pool(1)
+            down(last, 0)
+            add_resid(last, 0)
+            turn_z(last - 1)
+            empty_z(last - 1)
+            turn_pool(0, "turned")
+            turn_pool(1, "turned")
+            empty_pool(0)
+            quant_z(G - 1, 1)
+            quant_zt(last - 1)
+            down(last, 1)
+            quant_pool(0)
+            store_y(last - 2)
+            project(last - 1)
+            group_z(nc.vector.tensor_copy, G, 1)
+            add_resid(last, 1)
+            empty_pool(1)
+            quant_pool(1)
+            group_z(nc.scalar.copy, G, 0)
+            group_z(nc.vector.tensor_copy, G, 2)
+            turn_z(last)
+            empty_z(last)
+            turn_pool(2, "mixed")
+            empty_pool(2)
+            group_z(nc.scalar.copy, G, 3, slice(0, CHUNK // 2))
+            quant_z(G, 0)
+            gather(0, range(G))
+            quant_zt(last)
+            project(last)
+            quant_pool(2)
+            gather(0, range(G, GROUPS))
+            store_y(last - 1)
+            store_y(last)
+            gather(1, range(G))
+            group_z(nc.vector.tensor_copy, G, 3, slice(CHUNK // 2, CHUNK))
+            quant_z(G, 1)
+            gather(1, range(G, GROUPS))
+            store_c(nc.vector.tensor_copy, 0, 0)
+            store_c(nc.scalar.copy, 1, 0)
+            store_c(nc.vector.tensor_copy, 0, 1)
+            store_c(nc.scalar.copy, 1, 1)

@@ -28,8 +28,9 @@ HALF = 512
 HALVES = D // HALF
 CHUNK = HALF // 2
 SLOT_TILES = R // P
+BANKS = 8
 
-W_SPLIT = HALF // 2
+W_SPLIT = 320
 ALL = slice(0, F)
 LEFT, RIGHT = slice(0, F // 2), slice(F // 2, F)
 RELU_VECTOR, RELU_SCALAR = slice(0, 7 * F // 8), slice(7 * F // 8, F)
@@ -50,7 +51,7 @@ def tile_reglu_down_two_reads_s8_kernel(
     with ExitStack() as ctx:
         keep = ctx.enter_context(tc.tile_pool(name="keep", bufs=1))
         sb = ctx.enter_context(tc.tile_pool(name="sb", bufs=2))
-        psum = ctx.enter_context(tc.psum_pool(name="psum", bufs=2))
+        psum = ctx.enter_context(tc.psum_pool(name="psum", bufs=BANKS))
 
         w_codes = keep.tile([P, F_PASSES, D], U32, name="w_codes", align_bytes=64)
         w_scales = keep.tile([P, F_PASSES, D], U8, name="w_scales", align_bytes=64)
@@ -66,29 +67,29 @@ def tile_reglu_down_two_reads_s8_kernel(
         ident = keep.tile([P, P], F32, name="ident", align_bytes=64)
 
         gates, ups, resids, relus, hs, hbanks, hts, hcs, hss = {}, {}, {}, {}, {}, {}, {}, {}, {}
-        accs, zs, zbanks, zts, zcs, zss, ybanks = {}, {}, {}, {}, {}, {}, {}
+        accs, zs, zbanks, zts, zcs, zss, ybanks, ys = {}, {}, {}, {}, {}, {}, {}, {}
         wraws, wgs, zis, pbanks, pts, cbanks = {}, {}, {}, {}, {}, {}
 
 
         def load_gate(i, cols=ALL):
             if i < TILES:
                 if i not in gates:
-                    gates[i] = sb.tile([P, F], BF16, tag="gate", name="gate_sb", bufs=4, align_bytes=64)
+                    gates[i] = sb.tile([P, F], BF16, tag="gate", name="gate_sb", bufs=5, align_bytes=64)
                 nc.sync.dma_start(out=gates[i][:, cols], in_=gate_v[i // PACK][:, i % PACK, cols])
 
         def load_up(i, cols=ALL):
             if i < TILES:
                 if i not in ups:
-                    ups[i] = sb.tile([P, F], BF16, tag="up", name="up_sb", bufs=4, align_bytes=64)
+                    ups[i] = sb.tile([P, F], BF16, tag="up", name="up_sb", bufs=5, align_bytes=64)
                 nc.sync.dma_start(out=ups[i][:, cols], in_=up_v[i // PACK][:, i % PACK, cols])
 
         def load_resid(i):
             if i < TILES:
-                resids[i] = sb.tile([P, D], BF16, tag="resid", name="resid_sb", bufs=4, align_bytes=64)
+                resids[i] = sb.tile([P, D], BF16, tag="resid", name="resid_sb", bufs=6, align_bytes=64)
                 nc.sync.dma_start(out=resids[i][:], in_=resid_v[i // PACK][:, i % PACK, :])
 
         def load_w(g, h):
-            wraws[g, h] = sb.tile([P, PACK, HALF], BF16, tag="wraw", name="w_raw", bufs=8, align_bytes=64)
+            wraws[g, h] = sb.tile([P, PACK, HALF], BF16, tag="wraw", name="w_raw", bufs=6, align_bytes=64)
             nc.sync.dma_start(out=wraws[g, h][:], in_=w_v[g][:, :, h * HALF : (h + 1) * HALF])
 
         def load_head():
@@ -107,13 +108,19 @@ def tile_reglu_down_two_reads_s8_kernel(
             nc.sync.dma_start(out=code_bytes[:], in_=pool_bytes.rearrange("(a p) m -> p a m", p=P))
 
 
-        def group_w(g, h):
-            wgs[g, h] = sb.tile([P, HALF, PACK], BF16, tag="wg", name="w_grouped", bufs=3, align_bytes=64)
-            for copy, cols in ((nc.scalar.copy, slice(0, W_SPLIT)), (nc.vector.tensor_copy, slice(W_SPLIT, HALF))):
-                copy(
-                    out=wgs[g, h][:, cols, :].rearrange("p (c i) j -> p c j i", i=RUN),
-                    in_=wraws[g, h][:, :, cols].rearrange("p j (c i) -> p c j i", i=RUN),
-                )
+        def group_w(copy, g, h, cols):
+            if (g, h) not in wgs:
+                wgs[g, h] = sb.tile([P, HALF, PACK], BF16, tag="wg", name="w_grouped", bufs=3, align_bytes=64)
+            copy(
+                out=wgs[g, h][:, cols, :].rearrange("p (c i) j -> p c j i", i=RUN),
+                in_=wraws[g, h][:, :, cols].rearrange("p j (c i) -> p c j i", i=RUN),
+            )
+
+        def group_w_s(g, h, split=W_SPLIT):
+            group_w(nc.scalar.copy, g, h, slice(0, split))
+
+        def group_w_v(g, h, split=W_SPLIT):
+            group_w(nc.vector.tensor_copy, g, h, slice(split, HALF))
 
         def quant_w(g, h):
             cols = slice(h * HALF, (h + 1) * HALF)
@@ -152,7 +159,7 @@ def tile_reglu_down_two_reads_s8_kernel(
         def turn_h(i):
             words = hs[i][:].bitcast(F32)
             for b in range(2):
-                hbanks[i, b] = psum.tile([P, 2, 2, P], F32, tag="turned", name="h_turned", bufs=2)
+                hbanks[i, b] = psum.tile([P, 2, 2, P], F32, tag="bank", name="h_turned")
                 for gb in range(2):
                     for u in range(2):
                         w0 = u * (F // 4) + (2 * b + gb) * P
@@ -166,8 +173,8 @@ def tile_reglu_down_two_reads_s8_kernel(
             )
 
         def quant_h(i):
-            hcs[i] = sb.tile([P, F_PASSES * P], U32, tag="hc", name="h_codes", bufs=2, align_bytes=64)
-            hss[i] = sb.tile([P, F_PASSES * P], U8, tag="hs", name="h_scales", bufs=2, align_bytes=64)
+            hcs[i] = sb.tile([P, F_PASSES * P], U32, tag="hc", name="h_codes", bufs=4, align_bytes=64)
+            hss[i] = sb.tile([P, F_PASSES * P], U8, tag="hs", name="h_scales", bufs=4, align_bytes=64)
             nc.vector.quantize_mx(
                 out=hcs[i][:].bitcast(FP8X4),
                 scales=hss[i][:],
@@ -175,10 +182,11 @@ def tile_reglu_down_two_reads_s8_kernel(
             )
 
 
-        def down(i, h):
-            accs[i, h] = psum.tile([P, HALF], F32, tag="acc", name="z_acc", bufs=4)
+        def down(i, h, passes=range(F_PASSES)):
+            if (i, h) not in accs:
+                accs[i, h] = psum.tile([P, HALF], F32, tag="bank", name="z_acc")
             cols = slice(h * HALF, (h + 1) * HALF)
-            for g in range(F_PASSES):
+            for g in passes:
                 toks = slice(g * P, (g + 1) * P)
                 nc.tensor.matmul_mx(
                     out=accs[i, h][:],
@@ -206,7 +214,7 @@ def tile_reglu_down_two_reads_s8_kernel(
         def turn_z(i):
             G, t = divmod(i, PACK)
             words = zs[G][:, t, :].bitcast(F32)
-            zbanks[i] = psum.tile([P, HALVES, 2, P], F32, tag="mixed", name="z_turned", bufs=2)
+            zbanks[i] = psum.tile([P, HALVES, 2, P], F32, tag="bank", name="z_turned")
             for h in range(HALVES):
                 for u in range(2):
                     w0 = h * (HALF // 2) + u * P
@@ -226,7 +234,7 @@ def tile_reglu_down_two_reads_s8_kernel(
             )
 
         def project(i):
-            ybanks[i] = psum.tile([P, N], F32, tag="mixed", name="y_acc", bufs=2)
+            ybanks[i] = psum.tile([P, N], F32, tag="bank", name="y_acc")
             for h in range(HALVES):
                 toks = slice(h * P, (h + 1) * P)
                 nc.tensor.matmul_mx(
@@ -239,10 +247,16 @@ def tile_reglu_down_two_reads_s8_kernel(
                     stop=(h == HALVES - 1),
                 )
 
-        def store_y(i):
-            y_sb = sb.tile([P, N], F32, tag="y", name="y_sb", bufs=3, align_bytes=64)
-            nc.scalar.copy(out=y_sb[:], in_=ybanks[i][:])
-            nc.sync.dma_start(out=y_v[i // PACK][:, i % PACK, :], in_=y_sb[:])
+        def empty_y(i):
+            if i // 2 not in ys:
+                ys[i // 2] = sb.tile([P, 2, N], F32, tag="wraw", name="y_sb", bufs=6, align_bytes=64)
+            nc.scalar.copy(out=ys[i // 2][:, i % 2, :], in_=ybanks[i][:])
+
+        def store_y(first, count):
+            t = first % PACK
+            nc.sync.dma_start(
+                out=y_v[first // PACK][:, t : t + count, :], in_=ys[first // 2][:, first % 2 : first % 2 + count, :]
+            )
 
 
         def group_z(copy, G, c, cols=slice(0, CHUNK)):
@@ -264,20 +278,21 @@ def tile_reglu_down_two_reads_s8_kernel(
                 in_=zis[G, h][:].rearrange("p d t -> p (d t)"),
             )
 
-        def scale_pool(a):
+        def scale_pool(a, groups):
+            toks = slice(groups.start * K_PASS, groups.stop * K_PASS)
             nc.vector.tensor_tensor(
-                out=pool_bf[:, a, :], in0=code_bytes[:, a, :].bitcast(FP8), in1=scale_row[:], op=MULT
+                out=pool_bf[:, a, toks], in0=code_bytes[:, a, toks].bitcast(FP8), in1=scale_row[:, toks], op=MULT
             )
 
-        def turn_pool(G, tag):
-            pbanks[G] = psum.tile([P, SLOT_TILES, 2, P], F32, tag=tag, name="pool_turned", bufs=2)
+        def turn_pool(G):
+            pbanks[G] = psum.tile([P, SLOT_TILES, 2, P], F32, tag="bank", name="pool_turned")
             for a in range(SLOT_TILES):
                 words = pool_bf[:, a, G * K_PASS : (G + 1) * K_PASS].bitcast(F32)
                 for u in range(2):
                     nc.tensor.transpose(pbanks[G][:, a, u, :], words[:, u : K_PASS // 2 : 2], ident[:])
 
         def empty_pool(G):
-            pts[G] = sb.tile([P, SLOT_TILES, P, 2], F32, tag="zt", name="pool_grouped", bufs=2, align_bytes=64)
+            pts[G] = sb.tile([P, SLOT_TILES, P, 2], F32, tag="pt", name="pool_grouped", bufs=3, align_bytes=64)
             nc.scalar.copy(out=pts[G][:], in_=pbanks[G][:].rearrange("p a u r -> p a r u"))
 
         def quant_pool(G):
@@ -291,8 +306,7 @@ def tile_reglu_down_two_reads_s8_kernel(
             cols = slice(h * HALF, (h + 1) * HALF)
             for a in range(SLOT_TILES):
                 if (a, h) not in cbanks:
-                    tag, bufs = (("turned", 2), ("acc", 4))[h]
-                    cbanks[a, h] = psum.tile([P, HALF], F32, tag=tag, name="c_acc", bufs=bufs)
+                    cbanks[a, h] = psum.tile([P, HALF], F32, tag="bank", name="c_acc")
                 slots = slice(a * P, (a + 1) * P)
                 for G in groups:
                     nc.tensor.matmul_mx(
@@ -314,159 +328,203 @@ def tile_reglu_down_two_reads_s8_kernel(
             nc.sync.dma_start(out=out_c[a * P : (a + 1) * P, h * HALF : (h + 1) * HALF], in_=c_sb[:])
 
         with tc.manual_schedule():
-            load_w(0, 0)
-            load_w(1, 0)
-            load_gate(0, LEFT)
-            load_up(0, RIGHT)
-            load_gate(0, RIGHT)
-            load_w(2, 0)
-            load_up(0, LEFT)
-            load_w(3, 0)
-            load_w(0, 1)
-            load_gate(1)
-            load_w(1, 1)
-            load_up(1)
-            load_w(2, 1)
-            load_w(3, 1)
-            load_resid(0)
-            load_gate(2)
-            load_gate(3)
-            load_resid(1)
-            load_up(2)
-            load_head()
-            load_up(3)
             nc.vector.memset(head_sc[:].rearrange("p g n -> p (g n)").bitcast(I32), 0)
             make_identity(nc, ident[:])
 
-            group_w(0, 0)
-            group_w(1, 0)
-            relu_v(0, LEFT)
+            load_w(0, 0)
+            load_gate(0)
+            load_w(1, 0)
+            load_up(0)
+            load_w(2, 0)
+            load_gate(1)
+            load_w(3, 0)
+            load_up(1)
+            load_w(0, 1)
+            load_gate(2)
+            load_w(1, 1)
+            load_up(2)
+
+            group_w_s(0, 0)
+            group_w_v(0, 0)
+            relu_v(0, ALL)
             quant_w(0, 0)
-            relu_v(0, RIGHT)
-            quant_w(1, 0)
-            product(0, RIGHT)
-            group_w(2, 0)
-            product(0, LEFT)
+            group_w_s(1, 0)
+            group_w_v(1, 0)
+            load_w(2, 1)
+            product(0)
             turn_h(0)
-            quant_w(2, 0)
-            group_w(3, 0)
-            group_w(0, 1)
-            relu_v(1, ALL)
-            quant_w(3, 0)
-            quant_w(0, 1)
-            group_w(1, 1)
-            empty_h(0, 0)
-            empty_h(0, 1)
-            product(1)
-            turn_h(1)
-            group_w(2, 1)
-            quant_h(0)
+            quant_w(1, 0)
+            group_w_s(2, 0)
+            group_w_v(2, 0)
+            load_w(3, 1)
+            load_resid(0)
+            load_resid(1)
+            load_gate(3)
+            load_up(3)
+            load_head()
             load_gate(4)
+            load_up(4)
             load_head_scales()
             load_resid(2)
-            load_up(4)
-            empty_h(1, 0)
-            down(0, 0)
-            quant_w(2, 1)
-            empty_h(1, 1)
-            quant_w(1, 1)
-            quant_h(1)
-            group_w(3, 1)
-            relu_v(2, ALL)
-            relu_s(3, ALL)
+            empty_h(0, 0)
+            empty_h(0, 1)
+            relu_v(1, ALL)
+            quant_w(2, 0)
+            group_w_s(3, 0)
+            group_w_v(3, 0)
+            quant_h(0)
             load_gate(5)
-            load_gate(6)
             load_up(5)
-            quant_w(3, 1)
-            add_resid(0, 0)
-            product(2)
-            load_gate(7)
+            load_resid(3)
+            product(1)
+            turn_h(1)
+            quant_w(3, 0)
+            down(0, 0)
+            group_w_s(0, 1)
+            group_w_v(0, 1)
+            empty_h(1, 0)
+            empty_h(1, 1)
+            relu_v(2, ALL)
+            quant_w(0, 1)
+            group_w_s(1, 1)
+            group_w_v(1, 1)
+            quant_h(1)
             down(1, 0)
-            down(0, 1)
+            product(2)
+            turn_h(2)
+            quant_w(1, 1)
+            down(0, 1, range(0, 2))
+            down(1, 1, range(0, 2))
+            group_w_s(2, 1, 192)
+            group_w_v(2, 1, 192)
+            group_w_s(3, 1, 192)
+            group_w_v(3, 1, 192)
+            empty_h(2, 0)
+            empty_h(2, 1)
+            quant_w(2, 1)
+            quant_w(3, 1)
+            down(0, 1, range(2, 4))
+            down(1, 1, range(2, 4))
+            add_resid(0, 0)
+            quant_h(2)
+            down(2, 0)
             add_resid(0, 1)
-            load_up(6)
-            down(1, 1)
+            relu_s(3, RIGHT)
+            relu_v(3, LEFT)
+            product(3)
+            turn_z(0)
+            turn_h(3)
+            empty_z(0)
+            empty_h(3, 0)
+            empty_h(3, 1)
+            down(2, 1)
             add_resid(1, 0)
             add_resid(1, 1)
-
-            for s in range(1, TILES - 1):
-                product(s + 2)
-                if s == 3:
-                    store_y(0)
-                if s == TILES - 2:
-                    scale_pool(0)
-                turn_h(s + 1)
-                turn_z(s - 1)
-                load_resid(s + 2)
-                if s in (6, 8, 10):
-                    quant_z(*divmod((s - 6) // 2, HALVES))
-                empty_h(s + 1, 0)
-                empty_z(s - 1)
-                empty_h(s + 1, 1)
-                if s >= 3:
-                    store_y(s - 2)
-                if s == 2:
-                    project(0)
-                relu_v(s + 3, RELU_VECTOR)
-                quant_zt(s - 1)
-                if s >= 2:
-                    down(s, 0)
-                relu_s(s + 3, RELU_SCALAR)
-                if s >= 2:
-                    down(s, 1)
-                if s == 4:
-                    load_pool()
-                if s >= 2:
-                    project(s - 1)
-                    add_resid(s, 0)
-                quant_h(s + 1)
-                load_gate(s + 7)
-                load_up(s + 6)
-                if s >= 4:
-                    group_z(nc.scalar.copy, *divmod(s - 4, PACK))
-                if s >= 2:
-                    add_resid(s, 1)
+            quant_zt(0)
+            relu_v(4, ALL)
+            project(0)
+            turn_z(1)
+            quant_h(3)
+            product(4)
+            down(3, 0)
+            empty_y(0)
+            empty_z(1)
+            add_resid(2, 0)
+            add_resid(2, 1)
+            turn_h(4)
+            turn_z(2)
+            relu_s(5, RIGHT)
+            relu_v(5, LEFT)
+            quant_zt(1)
+            down(3, 1)
+            project(1)
+            empty_h(4, 0)
+            empty_h(4, 1)
+            product(5)
+            quant_h(4)
+            add_resid(3, 0)
+            load_gate(6)
+            load_up(6)
+            load_resid(4)
+            load_gate(7)
+            load_up(7)
+            load_resid(5)
+            relu_s(6, RIGHT)
+            relu_v(6, LEFT)
 
             last, G = TILES - 1, GROUPS - 1
-            group_z(nc.scalar.copy, G - 1, 3)
-            scale_pool(1)
-            down(last, 0)
-            add_resid(last, 0)
-            turn_z(last - 1)
-            empty_z(last - 1)
-            turn_pool(0, "turned")
-            turn_pool(1, "turned")
-            empty_pool(0)
-            quant_z(G - 1, 1)
-            quant_zt(last - 1)
-            down(last, 1)
-            quant_pool(0)
-            store_y(last - 2)
-            project(last - 1)
-            group_z(nc.vector.tensor_copy, G, 1)
+            for s in range(4, TILES):
+                if s > 4:
+                    turn_z(s - 2)
+                if s < last:
+                    turn_h(s + 1)
+                else:
+                    for g in range(GROUPS):
+                        turn_pool(g)
+                empty_y(s - 3)
+                empty_z(s - 2)
+                add_resid(s - 1, 1)
+                product(s + 2)
+                if s < last:
+                    empty_h(s + 1, 0)
+                    empty_h(s + 1, 1)
+                else:
+                    for g in range(GROUPS):
+                        empty_pool(g)
+                quant_zt(s - 2)
+                down(s, 0)
+                down(s, 1)
+                project(s - 2)
+                relu_v(s + 3, RELU_VECTOR)
+                relu_s(s + 3, RELU_SCALAR)
+                if s in (6, 8, 10):
+                    quant_z(*divmod((s - 6) // 2, HALVES))
+                if s == last - 1:
+                    scale_pool(1, range(GROUPS))
+                if s < last:
+                    quant_h(s + 1)
+                else:
+                    for g in range(GROUPS):
+                        quant_pool(g)
+                add_resid(s, 0)
+                if s == last - 2:
+                    scale_pool(0, range(GROUPS))
+                group_z(nc.scalar.copy, *divmod(s - 4, PACK))
+                load_gate(s + 4)
+                load_up(s + 4)
+                load_resid(s + 2)
+                if s + 4 == last:
+                    load_pool()
+                if s + 4 > last:
+                    store_y(2 * (s + 3 - last), 2)
+
+            group_z(nc.vector.tensor_copy, G, 0)
             add_resid(last, 1)
-            empty_pool(1)
-            quant_pool(1)
-            group_z(nc.scalar.copy, G, 0)
-            group_z(nc.vector.tensor_copy, G, 2)
+            turn_z(last - 1)
             turn_z(last)
+            empty_y(last - 2)
+            store_y(last - 3, 2)
+            empty_z(last - 1)
             empty_z(last)
-            turn_pool(2, "mixed")
-            empty_pool(2)
-            group_z(nc.scalar.copy, G, 3, slice(0, CHUNK // 2))
-            quant_z(G, 0)
+            group_z(nc.vector.tensor_copy, G, 1)
+            quant_z(G - 1, 1)
             gather(0, range(G))
+            quant_zt(last - 1)
+            project(last - 1)
+            quant_z(G, 0)
+            group_z(nc.scalar.copy, G, 2)
+            group_z(nc.vector.tensor_copy, G, 3)
             quant_zt(last)
-            project(last)
-            quant_pool(2)
             gather(0, range(G, GROUPS))
-            store_y(last - 1)
-            store_y(last)
+            project(last)
             gather(1, range(G))
-            group_z(nc.vector.tensor_copy, G, 3, slice(CHUNK // 2, CHUNK))
+            empty_y(last - 1)
+            store_y(last - 1, 1)
             quant_z(G, 1)
             gather(1, range(G, GROUPS))
-            store_c(nc.vector.tensor_copy, 0, 0)
-            store_c(nc.scalar.copy, 1, 0)
+            store_c(nc.scalar.copy, 0, 0)
+            store_c(nc.vector.tensor_copy, 1, 0)
+            empty_y(last)
+            store_y(last, 1)
             store_c(nc.vector.tensor_copy, 0, 1)
             store_c(nc.scalar.copy, 1, 1)

@@ -33,7 +33,7 @@ BANKS = 8
 W_SPLIT = 320
 ALL = slice(0, F)
 LEFT, RIGHT = slice(0, F // 2), slice(F // 2, F)
-RELU_VECTOR, RELU_SCALAR = slice(0, 7 * F // 8), slice(7 * F // 8, F)
+RELU_VECTOR, RELU_SCALAR = slice(0, 13 * F // 16), slice(13 * F // 16, F)
 RUN = 4
 
 
@@ -51,7 +51,16 @@ def tile_reglu_down_two_reads_s8_kernel(
     with ExitStack() as ctx:
         keep = ctx.enter_context(tc.tile_pool(name="keep", bufs=1))
         sb = ctx.enter_context(tc.tile_pool(name="sb", bufs=2))
-        psum = ctx.enter_context(tc.psum_pool(name="psum", bufs=BANKS))
+        psum = ctx.enter_context(tc.psum_pool(name="psum", bufs=1))
+        free_banks = list(range(BANKS))
+        bank_of = {}
+
+        def take_bank(name, key, shape):
+            bank_of[name, key] = free_banks.pop(0)
+            return psum.tile(shape, F32, tag="bank%d" % bank_of[name, key], name=name)
+
+        def give_bank(name, key):
+            free_banks.append(bank_of[name, key])
 
         w_codes = keep.tile([P, F_PASSES, D], U32, name="w_codes", align_bytes=64)
         w_scales = keep.tile([P, F_PASSES, D], U8, name="w_scales", align_bytes=64)
@@ -159,7 +168,7 @@ def tile_reglu_down_two_reads_s8_kernel(
         def turn_h(i):
             words = hs[i][:].bitcast(F32)
             for b in range(2):
-                hbanks[i, b] = psum.tile([P, 2, 2, P], F32, tag="bank", name="h_turned")
+                hbanks[i, b] = take_bank("h_turned", (i, b), [P, 2, 2, P])
                 for gb in range(2):
                     for u in range(2):
                         w0 = u * (F // 4) + (2 * b + gb) * P
@@ -171,6 +180,7 @@ def tile_reglu_down_two_reads_s8_kernel(
             nc.scalar.copy(
                 out=hts[i][:, 2 * b : 2 * b + 2, :, :], in_=hbanks[i, b][:].rearrange("p g u m -> p g m u")
             )
+            give_bank("h_turned", (i, b))
 
         def quant_h(i):
             hcs[i] = sb.tile([P, F_PASSES * P], U32, tag="hc", name="h_codes", bufs=4, align_bytes=64)
@@ -184,7 +194,7 @@ def tile_reglu_down_two_reads_s8_kernel(
 
         def down(i, h, passes=range(F_PASSES)):
             if (i, h) not in accs:
-                accs[i, h] = psum.tile([P, HALF], F32, tag="bank", name="z_acc")
+                accs[i, h] = take_bank("z_acc", (i, h), [P, HALF])
             cols = slice(h * HALF, (h + 1) * HALF)
             for g in passes:
                 toks = slice(g * P, (g + 1) * P)
@@ -209,12 +219,13 @@ def tile_reglu_down_two_reads_s8_kernel(
                 in1=resids[i][:, cols].rearrange("p (q u e) -> p u q e", u=2, e=2),
                 op=ADD,
             )
+            give_bank("z_acc", (i, h))
 
 
         def turn_z(i):
             G, t = divmod(i, PACK)
             words = zs[G][:, t, :].bitcast(F32)
-            zbanks[i] = psum.tile([P, HALVES, 2, P], F32, tag="bank", name="z_turned")
+            zbanks[i] = take_bank("z_turned", i, [P, HALVES, 2, P])
             for h in range(HALVES):
                 for u in range(2):
                     w0 = h * (HALF // 2) + u * P
@@ -223,6 +234,7 @@ def tile_reglu_down_two_reads_s8_kernel(
         def empty_z(i):
             zts[i] = sb.tile([P, HALVES, P, 2], F32, tag="zt", name="zt_grouped", bufs=2, align_bytes=64)
             nc.scalar.copy(out=zts[i][:], in_=zbanks[i][:].rearrange("p h u m -> p h m u"))
+            give_bank("z_turned", i)
 
         def quant_zt(i):
             zcs[i] = sb.tile([P, HALVES * P], U32, tag="ztc", name="zt_codes", bufs=2, align_bytes=64)
@@ -234,7 +246,7 @@ def tile_reglu_down_two_reads_s8_kernel(
             )
 
         def project(i):
-            ybanks[i] = psum.tile([P, N], F32, tag="bank", name="y_acc")
+            ybanks[i] = take_bank("y_acc", i, [P, N])
             for h in range(HALVES):
                 toks = slice(h * P, (h + 1) * P)
                 nc.tensor.matmul_mx(
@@ -251,6 +263,7 @@ def tile_reglu_down_two_reads_s8_kernel(
             if i // 2 not in ys:
                 ys[i // 2] = sb.tile([P, 2, N], F32, tag="wraw", name="y_sb", bufs=6, align_bytes=64)
             nc.scalar.copy(out=ys[i // 2][:, i % 2, :], in_=ybanks[i][:])
+            give_bank("y_acc", i)
 
         def store_y(first, count):
             t = first % PACK
@@ -262,7 +275,7 @@ def tile_reglu_down_two_reads_s8_kernel(
         def group_z(copy, G, c, cols=slice(0, CHUNK)):
             h, c0 = divmod(c * CHUNK, HALF)
             if (G, h) not in zis:
-                zis[G, h] = sb.tile([P, HALF, PACK], BF16, tag="zi", name="z_grouped", bufs=2, align_bytes=64)
+                zis[G, h] = sb.tile([P, HALF, PACK], BF16, tag="zi", name="z_grouped", bufs=3, align_bytes=64)
             copy(
                 out=zis[G, h][:, c0 + cols.start : c0 + cols.stop, :].rearrange("p (c i) t -> p c t i", i=RUN),
                 in_=zs[G][:, :, c * CHUNK + cols.start : c * CHUNK + cols.stop].rearrange(
@@ -285,7 +298,7 @@ def tile_reglu_down_two_reads_s8_kernel(
             )
 
         def turn_pool(G):
-            pbanks[G] = psum.tile([P, SLOT_TILES, 2, P], F32, tag="bank", name="pool_turned")
+            pbanks[G] = take_bank("pool_turned", G, [P, SLOT_TILES, 2, P])
             for a in range(SLOT_TILES):
                 words = pool_bf[:, a, G * K_PASS : (G + 1) * K_PASS].bitcast(F32)
                 for u in range(2):
@@ -294,6 +307,7 @@ def tile_reglu_down_two_reads_s8_kernel(
         def empty_pool(G):
             pts[G] = sb.tile([P, SLOT_TILES, P, 2], F32, tag="pt", name="pool_grouped", bufs=3, align_bytes=64)
             nc.scalar.copy(out=pts[G][:], in_=pbanks[G][:].rearrange("p a u r -> p a r u"))
+            give_bank("pool_turned", G)
 
         def quant_pool(G):
             nc.vector.quantize_mx(
@@ -302,30 +316,32 @@ def tile_reglu_down_two_reads_s8_kernel(
                 in_=pts[G][:].rearrange("p a r u -> p (a r u)").bitcast(BF16),
             )
 
-        def gather(h, groups):
+        def gather(a, h, groups):
+            if (a, h) not in cbanks:
+                cbanks[a, h] = take_bank("c_acc", (a, h), [P, HALF])
             cols = slice(h * HALF, (h + 1) * HALF)
-            for a in range(SLOT_TILES):
-                if (a, h) not in cbanks:
-                    cbanks[a, h] = psum.tile([P, HALF], F32, tag="bank", name="c_acc")
-                slots = slice(a * P, (a + 1) * P)
-                for G in groups:
-                    nc.tensor.matmul_mx(
-                        out=cbanks[a, h][:],
-                        lhsT=pool_codes[:, G, slots].bitcast(FP8X4),
-                        lhsT_scale=pool_scales[:, G, slots],
-                        rhs=z_codes[:, G, cols].bitcast(FP8X4),
-                        rhs_scale=z_scales[:, G, cols],
-                        start=(G == 0),
-                        stop=(G == GROUPS - 1),
-                    )
+            slots = slice(a * P, (a + 1) * P)
+            for G in groups:
+                nc.tensor.matmul_mx(
+                    out=cbanks[a, h][:],
+                    lhsT=pool_codes[:, G, slots].bitcast(FP8X4),
+                    lhsT_scale=pool_scales[:, G, slots],
+                    rhs=z_codes[:, G, cols].bitcast(FP8X4),
+                    rhs_scale=z_scales[:, G, cols],
+                    start=(G == 0),
+                    stop=(G == GROUPS - 1),
+                )
 
-        def store_c(copy, a, h):
-            c_sb = sb.tile([P, HALF], F32, tag="c", name="c_sb", bufs=4, align_bytes=64)
+        def store_c(copy, a, h, cols=slice(0, HALF)):
+            width = cols.stop - cols.start
+            c_sb = sb.tile([P, width], F32, tag="c", name="c_sb", bufs=6, align_bytes=64)
             copy(
                 out=c_sb[:].rearrange("p (q u e) -> p q u e", u=2, e=2),
-                in_=cbanks[a, h][:].rearrange("p (u q e) -> p q u e", u=2, e=2),
+                in_=cbanks[a, h][:].rearrange("p (u q e) -> p q u e", u=2, e=2)[:, cols.start // 4 : cols.stop // 4],
             )
-            nc.sync.dma_start(out=out_c[a * P : (a + 1) * P, h * HALF : (h + 1) * HALF], in_=c_sb[:])
+            nc.sync.dma_start(
+                out=out_c[a * P : (a + 1) * P, h * HALF + cols.start : h * HALF + cols.stop], in_=c_sb[:]
+            )
 
         with tc.manual_schedule():
             nc.vector.memset(head_sc[:].rearrange("p g n -> p (g n)").bitcast(I32), 0)
@@ -361,9 +377,9 @@ def tile_reglu_down_two_reads_s8_kernel(
             load_resid(1)
             load_gate(3)
             load_up(3)
-            load_head()
             load_gate(4)
             load_up(4)
+            load_head()
             load_head_scales()
             load_resid(2)
             empty_h(0, 0)
@@ -408,9 +424,9 @@ def tile_reglu_down_two_reads_s8_kernel(
             add_resid(0, 0)
             quant_h(2)
             down(2, 0)
-            add_resid(0, 1)
             relu_s(3, RIGHT)
             relu_v(3, LEFT)
+            add_resid(0, 1)
             product(3)
             turn_z(0)
             turn_h(3)
@@ -420,111 +436,102 @@ def tile_reglu_down_two_reads_s8_kernel(
             down(2, 1)
             add_resid(1, 0)
             add_resid(1, 1)
-            quant_zt(0)
             relu_v(4, ALL)
+            quant_zt(0)
             project(0)
-            turn_z(1)
-            quant_h(3)
             product(4)
-            down(3, 0)
-            empty_y(0)
-            empty_z(1)
+            quant_h(3)
             add_resid(2, 0)
-            add_resid(2, 1)
-            turn_h(4)
-            turn_z(2)
-            relu_s(5, RIGHT)
-            relu_v(5, LEFT)
-            quant_zt(1)
-            down(3, 1)
-            project(1)
-            empty_h(4, 0)
-            empty_h(4, 1)
-            product(5)
-            quant_h(4)
-            add_resid(3, 0)
             load_gate(6)
             load_up(6)
             load_resid(4)
-            load_gate(7)
-            load_up(7)
-            load_resid(5)
-            relu_s(6, RIGHT)
-            relu_v(6, LEFT)
 
             last, G = TILES - 1, GROUPS - 1
-            for s in range(4, TILES):
-                if s > 4:
-                    turn_z(s - 2)
-                if s < last:
-                    turn_h(s + 1)
-                else:
-                    for g in range(GROUPS):
-                        turn_pool(g)
+            pool_pieces = {last - 4: [(0, 0)], last - 2: [(1, 0)], last - 1: [(0, 1), (1, 1)]}
+            for s in range(3, last):
+                turn_z(s - 2)
+                turn_h(s + 1)
+                if s == last - 1:
+                    turn_pool(0)
                 empty_y(s - 3)
                 empty_z(s - 2)
+                relu_v(s + 2, RELU_VECTOR if s > 3 else ALL)
                 add_resid(s - 1, 1)
-                product(s + 2)
-                if s < last:
-                    empty_h(s + 1, 0)
-                    empty_h(s + 1, 1)
-                else:
-                    for g in range(GROUPS):
-                        empty_pool(g)
+                for a, g in pool_pieces.get(s, []):
+                    scale_pool(a, range(g, g + 1))
                 quant_zt(s - 2)
+                product(s + 2)
+                empty_h(s + 1, 0)
+                empty_h(s + 1, 1)
+                if s == last - 1:
+                    empty_pool(0)
                 down(s, 0)
                 down(s, 1)
                 project(s - 2)
-                relu_v(s + 3, RELU_VECTOR)
-                relu_s(s + 3, RELU_SCALAR)
                 if s in (6, 8, 10):
                     quant_z(*divmod((s - 6) // 2, HALVES))
+                quant_h(s + 1)
                 if s == last - 1:
-                    scale_pool(1, range(GROUPS))
-                if s < last:
-                    quant_h(s + 1)
-                else:
-                    for g in range(GROUPS):
-                        quant_pool(g)
+                    quant_pool(0)
                 add_resid(s, 0)
-                if s == last - 2:
-                    scale_pool(0, range(GROUPS))
-                group_z(nc.scalar.copy, *divmod(s - 4, PACK))
+                if s >= PACK:
+                    group_z(nc.scalar.copy, *divmod(s - PACK, PACK))
+                relu_s(s + 3, RELU_SCALAR)
                 load_gate(s + 4)
                 load_up(s + 4)
                 load_resid(s + 2)
-                if s + 4 == last:
+                if s == last - 6:
                     load_pool()
                 if s + 4 > last:
                     store_y(2 * (s + 3 - last), 2)
 
-            group_z(nc.vector.tensor_copy, G, 0)
-            add_resid(last, 1)
+            down(last, 0)
+            empty_y(last - 3)
+            store_y(last - 5, 2)
+            group_z(nc.scalar.copy, G - 1, 3)
+            add_resid(last - 1, 1)
+            scale_pool(0, range(G, GROUPS))
+            scale_pool(1, range(G, GROUPS))
+            turn_z(last - 2)
             turn_z(last - 1)
+            turn_pool(1)
+            turn_pool(G)
+            add_resid(last, 0)
+            empty_z(last - 2)
+            empty_z(last - 1)
+            empty_pool(1)
+            empty_pool(G)
+            down(last, 1)
+            quant_zt(last - 2)
+            project(last - 2)
+            group_z(nc.vector.tensor_copy, G, 0)
+            quant_zt(last - 1)
+            project(last - 1)
+            group_z(nc.vector.tensor_copy, G, 1)
+            add_resid(last, 1)
             turn_z(last)
             empty_y(last - 2)
             store_y(last - 3, 2)
-            empty_z(last - 1)
-            empty_z(last)
-            group_z(nc.vector.tensor_copy, G, 1)
-            quant_z(G - 1, 1)
-            gather(0, range(G))
-            quant_zt(last - 1)
-            project(last - 1)
-            quant_z(G, 0)
-            group_z(nc.scalar.copy, G, 2)
-            group_z(nc.vector.tensor_copy, G, 3)
-            quant_zt(last)
-            gather(0, range(G, GROUPS))
-            project(last)
-            gather(1, range(G))
             empty_y(last - 1)
             store_y(last - 1, 1)
+            empty_z(last)
+            group_z(nc.scalar.copy, G, 2, slice(0, CHUNK // 2))
+            quant_z(G, 0)
+            quant_pool(1)
+            quant_pool(G)
+            gather(0, 0, range(GROUPS))
+            gather(1, 0, range(GROUPS))
+            group_z(nc.vector.tensor_copy, G, 2, slice(CHUNK // 2, HALF))
+            quant_zt(last)
+            project(last)
+            quant_z(G - 1, 1)
             quant_z(G, 1)
-            gather(1, range(G, GROUPS))
+            gather(0, 1, range(GROUPS))
+            gather(1, 1, range(GROUPS))
             store_c(nc.scalar.copy, 0, 0)
-            store_c(nc.vector.tensor_copy, 1, 0)
+            store_c(nc.scalar.copy, 1, 0)
             empty_y(last)
             store_y(last, 1)
             store_c(nc.vector.tensor_copy, 0, 1)
-            store_c(nc.scalar.copy, 1, 1)
+            for cols in (slice(0, CHUNK), slice(CHUNK, HALF)):
+                store_c(nc.scalar.copy, 1, 1, cols)

@@ -62,18 +62,18 @@ def tile_reglu_down_two_reads_s8_kernel(
         def give_bank(name, key):
             free_banks.append(bank_of[name, key])
 
-        w_codes = keep.tile([P, F_PASSES, D], U32, name="w_codes", align_bytes=64)
-        w_scales = keep.tile([P, F_PASSES, D], U8, name="w_scales", align_bytes=64)
-        z_codes = keep.tile([P, GROUPS, D], U32, name="z_codes", align_bytes=64)
-        z_scales = keep.tile([P, GROUPS, D], U8, name="z_scales", align_bytes=64)
-        pool_codes = keep.tile([P, GROUPS, R], U32, name="pool_codes", align_bytes=64)
-        pool_scales = keep.tile([P, GROUPS, R], U8, name="pool_scales", align_bytes=64)
-        head_sb = keep.tile([P, HALVES, 2 * N], U8, name="head_sb", align_bytes=64)
-        head_sc = keep.tile([P, HALVES, N], U8, name="head_sc", align_bytes=64)
-        code_bytes = keep.tile([P, SLOT_TILES, M], U8, name="code_bytes", align_bytes=64)
-        scale_row = keep.tile([P, M], F32, name="scale_row", align_bytes=64)
-        pool_bf = keep.tile([P, SLOT_TILES, M], BF16, name="pool_bf", align_bytes=64)
-        ident = keep.tile([P, P], F32, name="ident", align_bytes=64)
+        w_codes = keep.tile([P, F_PASSES, D], U32, name="w_codes", align_bytes=256)
+        w_scales = keep.tile([P, F_PASSES, D], U8, name="w_scales", align_bytes=256)
+        z_codes = keep.tile([P, GROUPS, D], U32, name="z_codes", align_bytes=256)
+        z_scales = keep.tile([P, GROUPS, D], U8, name="z_scales", align_bytes=256)
+        pool_codes = keep.tile([P, GROUPS, R], U32, name="pool_codes", align_bytes=256)
+        pool_scales = keep.tile([P, GROUPS, R], U8, name="pool_scales", align_bytes=256)
+        head_sb = keep.tile([P, HALVES, 2 * N], U8, name="head_sb", align_bytes=256)
+        head_sc = keep.tile([P, HALVES, N], U8, name="head_sc", align_bytes=256)
+        code_bytes = keep.tile([P, SLOT_TILES, M], U8, name="code_bytes", align_bytes=256)
+        scale_row = keep.tile([P, M], F32, name="scale_row", align_bytes=256)
+        pool_bf = keep.tile([P, SLOT_TILES, M], BF16, name="pool_bf", align_bytes=256)
+        ident = keep.tile([P, P], F32, name="ident", align_bytes=256)
 
         gates, ups, resids, relus, hs, hbanks, hts, hcs, hss = {}, {}, {}, {}, {}, {}, {}, {}, {}
         accs, zs, zbanks, zts, zcs, zss, ybanks, ys = {}, {}, {}, {}, {}, {}, {}, {}
@@ -83,22 +83,22 @@ def tile_reglu_down_two_reads_s8_kernel(
         def load_gate(i, cols=ALL):
             if i < TILES:
                 if i not in gates:
-                    gates[i] = sb.tile([P, F], BF16, tag="gate", name="gate_sb", bufs=5, align_bytes=64)
+                    gates[i] = sb.tile([P, F], BF16, tag="gate", name="gate_sb", bufs=5, align_bytes=256)
                 nc.sync.dma_start(out=gates[i][:, cols], in_=gate_v[i // PACK][:, i % PACK, cols])
 
         def load_up(i, cols=ALL):
             if i < TILES:
                 if i not in ups:
-                    ups[i] = sb.tile([P, F], BF16, tag="up", name="up_sb", bufs=5, align_bytes=64)
+                    ups[i] = sb.tile([P, F], BF16, tag="up", name="up_sb", bufs=5, align_bytes=256)
                 nc.sync.dma_start(out=ups[i][:, cols], in_=up_v[i // PACK][:, i % PACK, cols])
 
         def load_resid(i):
             if i < TILES:
-                resids[i] = sb.tile([P, D], BF16, tag="resid", name="resid_sb", bufs=6, align_bytes=64)
+                resids[i] = sb.tile([P, D], BF16, tag="resid", name="resid_sb", bufs=6, align_bytes=256)
                 nc.sync.dma_start(out=resids[i][:], in_=resid_v[i // PACK][:, i % PACK, :])
 
         def load_w(g, h):
-            wraws[g, h] = sb.tile([P, PACK, HALF], BF16, tag="wraw", name="w_raw", bufs=6, align_bytes=64)
+            wraws[g, h] = sb.tile([P, PACK, HALF], BF16, tag="wraw", name="w_raw", bufs=6, align_bytes=256)
             nc.sync.dma_start(out=wraws[g, h][:], in_=w_v[g][:, :, h * HALF : (h + 1) * HALF])
 
         def load_head():
@@ -119,7 +119,7 @@ def tile_reglu_down_two_reads_s8_kernel(
 
         def group_w(copy, g, h, cols):
             if (g, h) not in wgs:
-                wgs[g, h] = sb.tile([P, HALF, PACK], BF16, tag="wg", name="w_grouped", bufs=3, align_bytes=64)
+                wgs[g, h] = sb.tile([P, HALF, PACK], BF16, tag="wg", name="w_grouped", bufs=3, align_bytes=256)
             copy(
                 out=wgs[g, h][:, cols, :].rearrange("p (c i) j -> p c j i", i=RUN),
                 in_=wraws[g, h][:, :, cols].rearrange("p j (c i) -> p c j i", i=RUN),
@@ -142,7 +142,7 @@ def tile_reglu_down_two_reads_s8_kernel(
 
         def relu_tile(i):
             if i not in relus:
-                relus[i] = sb.tile([P, F], BF16, tag="relu", name="relu_sb", bufs=2, align_bytes=64)
+                relus[i] = sb.tile([P, F], BF16, tag="relu", name="relu_sb", bufs=2, align_bytes=256)
             return relus[i]
 
         def relu_v(i, cols):
@@ -156,7 +156,7 @@ def tile_reglu_down_two_reads_s8_kernel(
         def product(i, cols=ALL):
             if i < TILES:
                 if i not in hs:
-                    hs[i] = sb.tile([P, F], BF16, tag="h", name="h_sb", bufs=2, align_bytes=64)
+                    hs[i] = sb.tile([P, F], BF16, tag="h", name="h_sb", bufs=2, align_bytes=256)
                 quads = slice(cols.start // 4, cols.stop // 4)
                 nc.vector.tensor_tensor(
                     out=hs[i][:].rearrange("p (u q e) -> p u q e", u=2, e=2)[:, :, quads, :],
@@ -176,15 +176,15 @@ def tile_reglu_down_two_reads_s8_kernel(
 
         def empty_h(i, b):
             if i not in hts:
-                hts[i] = sb.tile([P, F_PASSES, P, 2], F32, tag="ht", name="h_grouped", bufs=2, align_bytes=64)
+                hts[i] = sb.tile([P, F_PASSES, P, 2], F32, tag="ht", name="h_grouped", bufs=2, align_bytes=256)
             nc.scalar.copy(
                 out=hts[i][:, 2 * b : 2 * b + 2, :, :], in_=hbanks[i, b][:].rearrange("p g u m -> p g m u")
             )
             give_bank("h_turned", (i, b))
 
         def quant_h(i):
-            hcs[i] = sb.tile([P, F_PASSES * P], U32, tag="hc", name="h_codes", bufs=4, align_bytes=64)
-            hss[i] = sb.tile([P, F_PASSES * P], U8, tag="hs", name="h_scales", bufs=4, align_bytes=64)
+            hcs[i] = sb.tile([P, F_PASSES * P], U32, tag="hc", name="h_codes", bufs=4, align_bytes=256)
+            hss[i] = sb.tile([P, F_PASSES * P], U8, tag="hs", name="h_scales", bufs=4, align_bytes=256)
             nc.vector.quantize_mx(
                 out=hcs[i][:].bitcast(FP8X4),
                 scales=hss[i][:],
@@ -211,7 +211,7 @@ def tile_reglu_down_two_reads_s8_kernel(
         def add_resid(i, h):
             G, t = divmod(i, PACK)
             if G not in zs:
-                zs[G] = sb.tile([P, PACK, D], BF16, tag="z", name="z_sb", bufs=2, align_bytes=64)
+                zs[G] = sb.tile([P, PACK, D], BF16, tag="z", name="z_sb", bufs=2, align_bytes=256)
             cols = slice(h * HALF, (h + 1) * HALF)
             nc.vector.tensor_tensor(
                 out=zs[G][:, t, cols].rearrange("p (u q e) -> p u q e", u=2, e=2),
@@ -232,13 +232,13 @@ def tile_reglu_down_two_reads_s8_kernel(
                     nc.tensor.transpose(zbanks[i][:, h, u, :], words[:, w0 : w0 + P], ident[:])
 
         def empty_z(i):
-            zts[i] = sb.tile([P, HALVES, P, 2], F32, tag="zt", name="zt_grouped", bufs=2, align_bytes=64)
+            zts[i] = sb.tile([P, HALVES, P, 2], F32, tag="zt", name="zt_grouped", bufs=2, align_bytes=256)
             nc.scalar.copy(out=zts[i][:], in_=zbanks[i][:].rearrange("p h u m -> p h m u"))
             give_bank("z_turned", i)
 
         def quant_zt(i):
-            zcs[i] = sb.tile([P, HALVES * P], U32, tag="ztc", name="zt_codes", bufs=2, align_bytes=64)
-            zss[i] = sb.tile([P, HALVES * P], U8, tag="zts", name="zt_scales", bufs=2, align_bytes=64)
+            zcs[i] = sb.tile([P, HALVES * P], U32, tag="ztc", name="zt_codes", bufs=2, align_bytes=256)
+            zss[i] = sb.tile([P, HALVES * P], U8, tag="zts", name="zt_scales", bufs=2, align_bytes=256)
             nc.vector.quantize_mx(
                 out=zcs[i][:].bitcast(FP8X4),
                 scales=zss[i][:],
@@ -261,7 +261,7 @@ def tile_reglu_down_two_reads_s8_kernel(
 
         def empty_y(i):
             if i // 2 not in ys:
-                ys[i // 2] = sb.tile([P, 2, N], F32, tag="wraw", name="y_sb", bufs=6, align_bytes=64)
+                ys[i // 2] = sb.tile([P, 2, N], F32, tag="wraw", name="y_sb", bufs=6, align_bytes=256)
             nc.scalar.copy(out=ys[i // 2][:, i % 2, :], in_=ybanks[i][:])
             give_bank("y_acc", i)
 
@@ -275,7 +275,7 @@ def tile_reglu_down_two_reads_s8_kernel(
         def group_z(copy, G, c, cols=slice(0, CHUNK)):
             h, c0 = divmod(c * CHUNK, HALF)
             if (G, h) not in zis:
-                zis[G, h] = sb.tile([P, HALF, PACK], BF16, tag="zi", name="z_grouped", bufs=3, align_bytes=64)
+                zis[G, h] = sb.tile([P, HALF, PACK], BF16, tag="zi", name="z_grouped", bufs=3, align_bytes=256)
             copy(
                 out=zis[G, h][:, c0 + cols.start : c0 + cols.stop, :].rearrange("p (c i) t -> p c t i", i=RUN),
                 in_=zs[G][:, :, c * CHUNK + cols.start : c * CHUNK + cols.stop].rearrange(
@@ -305,7 +305,7 @@ def tile_reglu_down_two_reads_s8_kernel(
                     nc.tensor.transpose(pbanks[G][:, a, u, :], words[:, u : K_PASS // 2 : 2], ident[:])
 
         def empty_pool(G):
-            pts[G] = sb.tile([P, SLOT_TILES, P, 2], F32, tag="pt", name="pool_grouped", bufs=3, align_bytes=64)
+            pts[G] = sb.tile([P, SLOT_TILES, P, 2], F32, tag="pt", name="pool_grouped", bufs=3, align_bytes=256)
             nc.scalar.copy(out=pts[G][:], in_=pbanks[G][:].rearrange("p a u r -> p a r u"))
             give_bank("pool_turned", G)
 
@@ -334,7 +334,7 @@ def tile_reglu_down_two_reads_s8_kernel(
 
         def store_c(copy, a, h, cols=slice(0, HALF)):
             width = cols.stop - cols.start
-            c_sb = sb.tile([P, width], F32, tag="c", name="c_sb", bufs=6, align_bytes=64)
+            c_sb = sb.tile([P, width], F32, tag="c", name="c_sb", bufs=6, align_bytes=256)
             copy(
                 out=c_sb[:].rearrange("p (q u e) -> p q u e", u=2, e=2),
                 in_=cbanks[a, h][:].rearrange("p (u q e) -> p q u e", u=2, e=2)[:, cols.start // 4 : cols.stop // 4],

@@ -94,7 +94,7 @@ def tile_reglu_down_two_reads_s8_kernel(
 
         def load_resid(i):
             if i < TILES:
-                resids[i] = sb.tile([P, D], BF16, tag="resid", name="resid_sb", bufs=6, align_bytes=256)
+                resids[i] = sb.tile([P, D], BF16, tag="resid", name="resid_sb", bufs=5, align_bytes=256)
                 nc.sync.dma_start(out=resids[i][:], in_=resid_v[i // PACK][:, i % PACK, :])
 
         def load_w(g, h):
@@ -182,13 +182,15 @@ def tile_reglu_down_two_reads_s8_kernel(
             )
             give_bank("h_turned", (i, b))
 
-        def quant_h(i):
-            hcs[i] = sb.tile([P, F_PASSES * P], U32, tag="hc", name="h_codes", bufs=4, align_bytes=256)
-            hss[i] = sb.tile([P, F_PASSES * P], U8, tag="hs", name="h_scales", bufs=4, align_bytes=256)
+        def quant_h(i, passes=slice(0, F_PASSES)):
+            if i not in hcs:
+                hcs[i] = sb.tile([P, F_PASSES * P], U32, tag="hc", name="h_codes", bufs=4, align_bytes=256)
+                hss[i] = sb.tile([P, F_PASSES * P], U8, tag="hs", name="h_scales", bufs=4, align_bytes=256)
+            toks = slice(passes.start * P, passes.stop * P)
             nc.vector.quantize_mx(
-                out=hcs[i][:].bitcast(FP8X4),
-                scales=hss[i][:],
-                in_=hts[i][:].rearrange("p g m u -> p (g m u)").bitcast(BF16),
+                out=hcs[i][:, toks].bitcast(FP8X4),
+                scales=hss[i][:, toks],
+                in_=hts[i][:, passes, :, :].rearrange("p g m u -> p (g m u)").bitcast(BF16),
             )
 
 
@@ -232,13 +234,13 @@ def tile_reglu_down_two_reads_s8_kernel(
                     nc.tensor.transpose(zbanks[i][:, h, u, :], words[:, w0 : w0 + P], ident[:])
 
         def empty_z(i):
-            zts[i] = sb.tile([P, HALVES, P, 2], F32, tag="zt", name="zt_grouped", bufs=2, align_bytes=256)
+            zts[i] = sb.tile([P, HALVES, P, 2], F32, tag="zt", name="zt_grouped", bufs=3, align_bytes=256)
             nc.scalar.copy(out=zts[i][:], in_=zbanks[i][:].rearrange("p h u m -> p h m u"))
             give_bank("z_turned", i)
 
         def quant_zt(i):
-            zcs[i] = sb.tile([P, HALVES * P], U32, tag="ztc", name="zt_codes", bufs=2, align_bytes=256)
-            zss[i] = sb.tile([P, HALVES * P], U8, tag="zts", name="zt_scales", bufs=2, align_bytes=256)
+            zcs[i] = sb.tile([P, HALVES * P], U32, tag="ztc", name="zt_codes", bufs=3, align_bytes=256)
+            zss[i] = sb.tile([P, HALVES * P], U8, tag="zts", name="zt_scales", bufs=3, align_bytes=256)
             nc.vector.quantize_mx(
                 out=zcs[i][:].bitcast(FP8X4),
                 scales=zss[i][:],
@@ -334,7 +336,7 @@ def tile_reglu_down_two_reads_s8_kernel(
 
         def store_c(copy, a, h, cols=slice(0, HALF)):
             width = cols.stop - cols.start
-            c_sb = sb.tile([P, width], F32, tag="c", name="c_sb", bufs=6, align_bytes=256)
+            c_sb = sb.tile([P, width], F32, tag="c", name="c_sb", bufs=5, align_bytes=256)
             copy(
                 out=c_sb[:].rearrange("p (q u e) -> p q u e", u=2, e=2),
                 in_=cbanks[a, h][:].rearrange("p (u q e) -> p q u e", u=2, e=2)[:, cols.start // 4 : cols.stop // 4],
@@ -447,86 +449,165 @@ def tile_reglu_down_two_reads_s8_kernel(
             load_resid(4)
 
             last, G = TILES - 1, GROUPS - 1
-            pool_pieces = {last - 4: [(0, 0)], last - 2: [(1, 0)], last - 1: [(0, 1), (1, 1)]}
-            for s in range(3, last):
-                turn_z(s - 2)
-                turn_h(s + 1)
-                if s == last - 1:
-                    turn_pool(0)
-                empty_y(s - 3)
-                empty_z(s - 2)
-                relu_v(s + 2, RELU_VECTOR if s > 3 else ALL)
-                add_resid(s - 1, 1)
-                for a, g in pool_pieces.get(s, []):
-                    scale_pool(a, range(g, g + 1))
-                quant_zt(s - 2)
-                product(s + 2)
-                empty_h(s + 1, 0)
-                empty_h(s + 1, 1)
-                if s == last - 1:
-                    empty_pool(0)
-                down(s, 0)
-                down(s, 1)
-                project(s - 2)
-                if s in (6, 8, 10):
-                    quant_z(*divmod((s - 6) // 2, HALVES))
-                quant_h(s + 1)
-                if s == last - 1:
-                    quant_pool(0)
-                add_resid(s, 0)
-                if s >= PACK:
-                    group_z(nc.scalar.copy, *divmod(s - PACK, PACK))
-                relu_s(s + 3, RELU_SCALAR)
-                load_gate(s + 4)
-                load_up(s + 4)
-                load_resid(s + 2)
-                if s == last - 6:
-                    load_pool()
-                if s + 4 > last:
-                    store_y(2 * (s + 3 - last), 2)
+
+            turn_z(1)
+            turn_h(4)
+            empty_y(0)
+            empty_z(1)
+            relu_v(5, ALL)
+            add_resid(2, 1)
+            quant_zt(1)
+            product(5)
+            empty_h(4, 0)
+            empty_h(4, 1)
+            down(3, 0)
+            down(3, 1)
+            project(1)
+            quant_h(4)
+            add_resid(3, 0)
+            relu_s(6, RELU_SCALAR)
+            load_gate(7)
+            load_up(7)
+            load_resid(5)
+
+            for i in (4, 5):
+                load_gate(i + 4)
+                load_up(i + 4)
+                load_resid(i + 2)
+            load_pool()
+            turn_z(2)
+            turn_h(5)
+            empty_y(1)
+            empty_z(2)
+            relu_v(6, RELU_VECTOR)
+            add_resid(3, 1)
+            quant_zt(2)
+            product(6)
+            empty_h(5, 0)
+            empty_h(5, 1)
+            down(4, 0)
+            down(4, 1)
+            project(2)
+            quant_h(5)
+            add_resid(4, 0)
+            relu_s(7, RELU_SCALAR)
+            group_z(nc.scalar.copy, 0, 0)
+            empty_y(2)
+            down(5, 0)
+            down(5, 1)
+            relu_v(7, RELU_VECTOR)
+            add_resid(4, 1)
+            product(7)
+            add_resid(5, 0)
+            group_z(nc.scalar.copy, 0, 1)
+            relu_s(8, RELU_SCALAR)
+
+            for a in range(6, last, 2):
+                for i in (a, a + 1):
+                    load_gate(i + 4)
+                    load_up(i + 4)
+                    load_resid(i + 2)
+                turn_h(a)
+                turn_h(a + 1)
+                add_resid(a - 1, 1)
+                if a == 6:
+                    turn_z(a - 3)
+                turn_z(a - 2)
+                relu_v(a + 2, RELU_VECTOR)
+                empty_h(a, 0)
+                empty_h(a, 1)
+                turn_z(a - 1)
+                quant_h(a, slice(0, 2))
+                quant_z(*divmod((a - 6) // 2, HALVES))
+                quant_h(a, slice(2, 4))
+                if a > 6:
+                    project(a - 3)
+                empty_h(a + 1, 0)
+                empty_h(a + 1, 1)
+                if a == 6:
+                    empty_z(a - 3)
+                empty_z(a - 2)
+                empty_z(a - 1)
+                down(a, 0)
+                down(a, 1)
+                product(a + 2)
+                if a == last - 1:
+                    scale_pool(0, range(1, 2))
+                    scale_pool(1, range(1, 2))
+                if a == 6:
+                    quant_zt(a - 3)
+                    project(a - 3)
+                quant_zt(a - 2)
+                project(a - 2)
+                quant_h(a + 1)
+                if a > 6:
+                    empty_y(a - 3)
+                add_resid(a, 0)
+                relu_s(a + 3, RELU_SCALAR)
+                group_z(nc.scalar.copy, *divmod(a - PACK, PACK))
+                if a == 6:
+                    empty_y(a - 3)
+                empty_y(a - 2)
+                if a + 1 < last:
+                    down(a + 1, 0)
+                    down(a + 1, 1)
+                    relu_v(a + 3, RELU_VECTOR)
+                    add_resid(a, 1)
+                    product(a + 3)
+                    quant_zt(a - 1)
+                    scale_pool((a - 6) // 2, range(0, 1))
+                    add_resid(a + 1, 0)
+                    group_z(nc.scalar.copy, *divmod(a + 1 - PACK, PACK))
+                    relu_s(a + 4, RELU_SCALAR)
+                store_y(a - 6, 2)
 
             down(last, 0)
-            empty_y(last - 3)
             store_y(last - 5, 2)
-            group_z(nc.scalar.copy, G - 1, 3)
-            add_resid(last - 1, 1)
-            scale_pool(0, range(G, GROUPS))
-            scale_pool(1, range(G, GROUPS))
-            turn_z(last - 2)
-            turn_z(last - 1)
-            turn_pool(1)
-            turn_pool(G)
-            add_resid(last, 0)
-            empty_z(last - 2)
-            empty_z(last - 1)
-            empty_pool(1)
-            empty_pool(G)
-            down(last, 1)
+            store_y(last - 3, 1)
             quant_zt(last - 2)
             project(last - 2)
+            add_resid(last - 1, 1)
+            group_z(nc.scalar.copy, G - 1, 3)
+            scale_pool(0, range(G, GROUPS))
+            turn_z(last - 1)
+            turn_pool(0)
+            turn_pool(1)
+            add_resid(last, 0)
+            scale_pool(1, range(G, GROUPS))
+            empty_y(last - 2)
+            store_y(last - 2, 1)
+            empty_z(last - 1)
+            empty_pool(0)
+            empty_pool(1)
+            down(last, 1)
             group_z(nc.vector.tensor_copy, G, 0)
+            quant_z(G - 1, 1)
             quant_zt(last - 1)
             project(last - 1)
-            group_z(nc.vector.tensor_copy, G, 1)
+            group_z(nc.scalar.copy, G, 1)
+            quant_pool(0)
+            quant_pool(1)
             add_resid(last, 1)
+            turn_pool(G)
             turn_z(last)
-            empty_y(last - 2)
-            store_y(last - 3, 2)
             empty_y(last - 1)
             store_y(last - 1, 1)
+            empty_pool(G)
             empty_z(last)
-            group_z(nc.scalar.copy, G, 2, slice(0, CHUNK // 2))
             quant_z(G, 0)
-            quant_pool(1)
+            gather(0, 0, range(G))
+            gather(1, 0, range(G))
+            gather(0, 1, range(1))
+            group_z(nc.vector.tensor_copy, G, 2)
             quant_pool(G)
-            gather(0, 0, range(GROUPS))
-            gather(1, 0, range(GROUPS))
-            group_z(nc.vector.tensor_copy, G, 2, slice(CHUNK // 2, HALF))
+            gather(0, 0, range(G, GROUPS))
+            gather(1, 0, range(G, GROUPS))
+            group_z(nc.vector.tensor_copy, G, 3)
             quant_zt(last)
-            project(last)
-            quant_z(G - 1, 1)
             quant_z(G, 1)
-            gather(0, 1, range(GROUPS))
+            gather(0, 1, range(1, G))
+            project(last)
+            gather(0, 1, range(G, GROUPS))
             gather(1, 1, range(GROUPS))
             store_c(nc.scalar.copy, 0, 0)
             store_c(nc.scalar.copy, 1, 0)

@@ -34,6 +34,7 @@ W_SPLIT = 320
 ALL = slice(0, F)
 LEFT, RIGHT = slice(0, F // 2), slice(F // 2, F)
 RELU_VECTOR, RELU_SCALAR = slice(0, 13 * F // 16), slice(13 * F // 16, F)
+TAIL_SPLIT = 192
 RUN = 4
 
 
@@ -430,102 +431,63 @@ def tile_reglu_down_two_reads_s8_kernel(
             relu_v(3, LEFT)
             add_resid(0, 1)
             product(3)
+            add_resid(1, 0)
+            add_resid(1, 1)
             turn_z(0)
             turn_h(3)
+            turn_z(1)
             empty_z(0)
             empty_h(3, 0)
             empty_h(3, 1)
+            empty_z(1)
             down(2, 1)
-            add_resid(1, 0)
-            add_resid(1, 1)
             relu_v(4, ALL)
             quant_zt(0)
             project(0)
-            product(4)
+            product(4, LEFT)
             quant_h(3)
+            product(4, RIGHT)
+            down(3, 0)
+            down(3, 1)
             add_resid(2, 0)
-            load_gate(6)
-            load_up(6)
-            load_resid(4)
-
-            last, G = TILES - 1, GROUPS - 1
-
-            turn_z(1)
-            turn_h(4)
+            relu_s(5, RIGHT)
             empty_y(0)
-            empty_z(1)
-            relu_v(5, ALL)
+            relu_v(5, LEFT)
             add_resid(2, 1)
             quant_zt(1)
             product(5)
-            empty_h(4, 0)
-            empty_h(4, 1)
-            down(3, 0)
-            down(3, 1)
-            project(1)
-            quant_h(4)
             add_resid(3, 0)
-            relu_s(6, RELU_SCALAR)
+            load_gate(6)
+            load_up(6)
+            load_resid(4)
             load_gate(7)
             load_up(7)
             load_resid(5)
+            relu_s(6, RELU_SCALAR)
+            last, G = TILES - 1, GROUPS - 1
 
-            for i in (4, 5):
-                load_gate(i + 4)
-                load_up(i + 4)
-                load_resid(i + 2)
-            load_pool()
-            turn_z(2)
-            turn_h(5)
-            empty_y(1)
-            empty_z(2)
-            relu_v(6, RELU_VECTOR)
-            add_resid(3, 1)
-            quant_zt(2)
-            product(6)
-            empty_h(5, 0)
-            empty_h(5, 1)
-            down(4, 0)
-            down(4, 1)
-            project(2)
-            quant_h(5)
-            add_resid(4, 0)
-            relu_s(7, RELU_SCALAR)
-            group_z(nc.scalar.copy, 0, 0)
-            empty_y(2)
-            down(5, 0)
-            down(5, 1)
-            relu_v(7, RELU_VECTOR)
-            add_resid(4, 1)
-            product(7)
-            add_resid(5, 0)
-            group_z(nc.scalar.copy, 0, 1)
-            relu_s(8, RELU_SCALAR)
-
-            for a in range(6, last, 2):
+            for a in range(4, last, 2):
                 for i in (a, a + 1):
                     load_gate(i + 4)
                     load_up(i + 4)
                     load_resid(i + 2)
+                if a == 4:
+                    load_pool()
                 turn_h(a)
+                turn_z(a - 2)
                 turn_h(a + 1)
                 add_resid(a - 1, 1)
-                if a == 6:
-                    turn_z(a - 3)
-                turn_z(a - 2)
                 relu_v(a + 2, RELU_VECTOR)
                 empty_h(a, 0)
                 empty_h(a, 1)
                 turn_z(a - 1)
                 quant_h(a, slice(0, 2))
-                quant_z(*divmod((a - 6) // 2, HALVES))
+                if a >= 6:
+                    quant_z(*divmod((a - 6) // 2, HALVES))
                 quant_h(a, slice(2, 4))
-                if a > 6:
-                    project(a - 3)
+                project(a - 3)
                 empty_h(a + 1, 0)
                 empty_h(a + 1, 1)
-                if a == 6:
-                    empty_z(a - 3)
                 empty_z(a - 2)
                 empty_z(a - 1)
                 down(a, 0)
@@ -534,19 +496,13 @@ def tile_reglu_down_two_reads_s8_kernel(
                 if a == last - 1:
                     scale_pool(0, range(1, 2))
                     scale_pool(1, range(1, 2))
-                if a == 6:
-                    quant_zt(a - 3)
-                    project(a - 3)
                 quant_zt(a - 2)
                 project(a - 2)
                 quant_h(a + 1)
-                if a > 6:
-                    empty_y(a - 3)
+                empty_y(a - 3)
                 add_resid(a, 0)
                 relu_s(a + 3, RELU_SCALAR)
                 group_z(nc.scalar.copy, *divmod(a - PACK, PACK))
-                if a == 6:
-                    empty_y(a - 3)
                 empty_y(a - 2)
                 if a + 1 < last:
                     down(a + 1, 0)
@@ -555,13 +511,16 @@ def tile_reglu_down_two_reads_s8_kernel(
                     add_resid(a, 1)
                     product(a + 3)
                     quant_zt(a - 1)
-                    scale_pool((a - 6) // 2, range(0, 1))
+                    if a >= 6:
+                        scale_pool((a - 6) // 2, range(0, 1))
                     add_resid(a + 1, 0)
                     group_z(nc.scalar.copy, *divmod(a + 1 - PACK, PACK))
                     relu_s(a + 4, RELU_SCALAR)
-                store_y(a - 6, 2)
+                if a >= 6:
+                    store_y(a - 6, 2)
 
             down(last, 0)
+            down(last, 1)
             store_y(last - 5, 2)
             store_y(last - 3, 1)
             quant_zt(last - 2)
@@ -569,46 +528,43 @@ def tile_reglu_down_two_reads_s8_kernel(
             add_resid(last - 1, 1)
             group_z(nc.scalar.copy, G - 1, 3)
             scale_pool(0, range(G, GROUPS))
+            add_resid(last, 0)
+            group_z(nc.scalar.copy, G, 0, slice(0, TAIL_SPLIT))
+            scale_pool(1, range(G, GROUPS))
+            add_resid(last, 1)
             turn_z(last - 1)
             turn_pool(0)
             turn_pool(1)
-            add_resid(last, 0)
-            scale_pool(1, range(G, GROUPS))
             empty_y(last - 2)
             store_y(last - 2, 1)
             empty_z(last - 1)
+            turn_z(last)
+            turn_pool(G)
             empty_pool(0)
             empty_pool(1)
-            down(last, 1)
-            group_z(nc.vector.tensor_copy, G, 0)
+            empty_pool(G)
+            empty_z(last)
+            group_z(nc.vector.tensor_copy, G, 0, slice(TAIL_SPLIT, HALF))
             quant_z(G - 1, 1)
             quant_zt(last - 1)
             project(last - 1)
-            group_z(nc.scalar.copy, G, 1)
+            quant_z(G, 0)
             quant_pool(0)
             quant_pool(1)
-            add_resid(last, 1)
-            turn_pool(G)
-            turn_z(last)
-            empty_y(last - 1)
-            store_y(last - 1, 1)
-            empty_pool(G)
-            empty_z(last)
-            quant_z(G, 0)
-            gather(0, 0, range(G))
-            gather(1, 0, range(G))
-            gather(0, 1, range(1))
             group_z(nc.vector.tensor_copy, G, 2)
             quant_pool(G)
-            gather(0, 0, range(G, GROUPS))
-            gather(1, 0, range(G, GROUPS))
+            for g in range(GROUPS):
+                gather(0, 0, range(g, g + 1))
+                gather(1, 0, range(g, g + 1))
             group_z(nc.vector.tensor_copy, G, 3)
             quant_zt(last)
             quant_z(G, 1)
-            gather(0, 1, range(1, G))
+            gather(0, 1, range(1))
             project(last)
-            gather(0, 1, range(G, GROUPS))
+            gather(0, 1, range(1, GROUPS))
             gather(1, 1, range(GROUPS))
+            empty_y(last - 1)
+            store_y(last - 1, 1)
             store_c(nc.scalar.copy, 0, 0)
             store_c(nc.scalar.copy, 1, 0)
             empty_y(last)

@@ -33,8 +33,9 @@ BANKS = 8
 W_SPLIT = 320
 ALL = slice(0, F)
 LEFT, RIGHT = slice(0, F // 2), slice(F // 2, F)
-RELU_VECTOR, RELU_SCALAR = slice(0, 13 * F // 16), slice(13 * F // 16, F)
-TAIL_SPLIT = 192
+RELU_VECTOR, RELU_SCALAR = slice(0, 5 * F // 8), slice(5 * F // 8, F)
+UP_SLOTS = 5
+BESIDE_ADDS = 192
 RUN = 4
 
 
@@ -90,7 +91,7 @@ def tile_reglu_down_two_reads_s8_kernel(
         def load_up(i, cols=ALL):
             if i < TILES:
                 if i not in ups:
-                    ups[i] = sb.tile([P, F], BF16, tag="up", name="up_sb", bufs=5, align_bytes=256)
+                    ups[i] = sb.tile([P, F], BF16, tag="up%d" % (i % UP_SLOTS), name="up_sb", bufs=1, align_bytes=256)
                 nc.sync.dma_start(out=ups[i][:, cols], in_=up_v[i // PACK][:, i % PACK, cols])
 
         def load_resid(i):
@@ -275,23 +276,37 @@ def tile_reglu_down_two_reads_s8_kernel(
             )
 
 
+        def z_chunk(G, c, tag="zi", bufs=4):
+            zis[G, c] = sb.tile([P, CHUNK, PACK], BF16, tag=tag, name="z_grouped", bufs=bufs, align_bytes=256)
+
         def group_z(copy, G, c, cols=slice(0, CHUNK)):
-            h, c0 = divmod(c * CHUNK, HALF)
-            if (G, h) not in zis:
-                zis[G, h] = sb.tile([P, HALF, PACK], BF16, tag="zi", name="z_grouped", bufs=3, align_bytes=256)
+            if (G, c) not in zis:
+                z_chunk(G, c)
             copy(
-                out=zis[G, h][:, c0 + cols.start : c0 + cols.stop, :].rearrange("p (c i) t -> p c t i", i=RUN),
+                out=zis[G, c][:, cols, :].rearrange("p (c i) t -> p c t i", i=RUN),
                 in_=zs[G][:, :, c * CHUNK + cols.start : c * CHUNK + cols.stop].rearrange(
                     "p t (c i) -> p c t i", i=RUN
                 ),
             )
 
-        def quant_z(G, h):
-            cols = slice(h * HALF, (h + 1) * HALF)
+        def group_z_beside_adds(i, G, c):
+            z_chunk(G, c, "up%d" % (i % UP_SLOTS), 1)
+            nc.gpsimd.tensor_scalar(
+                out=zis[G, c][:, :BESIDE_ADDS, :],
+                in0=zs[G][:, :, c * CHUNK : c * CHUNK + BESIDE_ADDS].rearrange("p t c -> p c t"),
+                scalar1=1.0,
+                scalar2=0.0,
+                op0=MULT,
+                op1=ADD,
+            )
+            group_z(nc.scalar.copy, G, c, slice(BESIDE_ADDS, CHUNK))
+
+        def quant_z(G, c):
+            cols = slice(c * CHUNK, (c + 1) * CHUNK)
             nc.vector.quantize_mx(
                 out=z_codes[:, G, cols].bitcast(FP8X4),
                 scales=z_scales[:, G, cols],
-                in_=zis[G, h][:].rearrange("p d t -> p (d t)"),
+                in_=zis[G, c][:].rearrange("p d t -> p (d t)"),
             )
 
         def scale_pool(a, groups):
@@ -463,28 +478,32 @@ def tile_reglu_down_two_reads_s8_kernel(
             load_gate(7)
             load_up(7)
             load_resid(5)
-            relu_s(6, RELU_SCALAR)
+            relu_s(6, slice(13 * F // 16, F))
             last, G = TILES - 1, GROUPS - 1
 
             for a in range(4, last, 2):
-                for i in (a, a + 1):
-                    load_gate(i + 4)
-                    load_up(i + 4)
-                    load_resid(i + 2)
+                load_gate(a + 4)
+                load_up(a + 4)
+                load_resid(a + 2)
+                load_gate(a + 5)
+                load_resid(a + 3)
+                load_up(a + 5)
                 if a == 4:
                     load_pool()
                 turn_h(a)
                 turn_z(a - 2)
                 turn_h(a + 1)
                 add_resid(a - 1, 1)
-                relu_v(a + 2, RELU_VECTOR)
+                relu_v(a + 2, RELU_VECTOR if a > 4 else slice(0, 13 * F // 16))
                 empty_h(a, 0)
                 empty_h(a, 1)
                 turn_z(a - 1)
                 quant_h(a, slice(0, 2))
                 if a >= 6:
-                    quant_z(*divmod((a - 6) // 2, HALVES))
+                    quant_z(*divmod(a - 6, PACK))
                 quant_h(a, slice(2, 4))
+                if a >= 6:
+                    quant_z(*divmod(a - 5, PACK))
                 project(a - 3)
                 empty_h(a + 1, 0)
                 empty_h(a + 1, 1)
@@ -492,16 +511,16 @@ def tile_reglu_down_two_reads_s8_kernel(
                 empty_z(a - 1)
                 down(a, 0)
                 down(a, 1)
-                product(a + 2)
                 if a == last - 1:
                     scale_pool(0, range(1, 2))
                     scale_pool(1, range(1, 2))
+                product(a + 2)
+                empty_y(a - 3)
+                relu_s(a + 3, RELU_SCALAR)
                 quant_zt(a - 2)
                 project(a - 2)
                 quant_h(a + 1)
-                empty_y(a - 3)
                 add_resid(a, 0)
-                relu_s(a + 3, RELU_SCALAR)
                 group_z(nc.scalar.copy, *divmod(a - PACK, PACK))
                 empty_y(a - 2)
                 if a + 1 < last:
@@ -509,16 +528,15 @@ def tile_reglu_down_two_reads_s8_kernel(
                     down(a + 1, 1)
                     relu_v(a + 3, RELU_VECTOR)
                     add_resid(a, 1)
-                    product(a + 3)
-                    quant_zt(a - 1)
                     if a >= 6:
                         scale_pool((a - 6) // 2, range(0, 1))
-                    add_resid(a + 1, 0)
-                    group_z(nc.scalar.copy, *divmod(a + 1 - PACK, PACK))
+                    product(a + 3)
+                    group_z_beside_adds(a + 3, *divmod(a + 1 - PACK, PACK))
                     relu_s(a + 4, RELU_SCALAR)
+                    quant_zt(a - 1)
+                    add_resid(a + 1, 0)
                 if a >= 6:
                     store_y(a - 6, 2)
-
             down(last, 0)
             down(last, 1)
             store_y(last - 5, 2)
@@ -528,15 +546,14 @@ def tile_reglu_down_two_reads_s8_kernel(
             add_resid(last - 1, 1)
             group_z(nc.scalar.copy, G - 1, 3)
             scale_pool(0, range(G, GROUPS))
+            quant_z(G - 1, 2)
             add_resid(last, 0)
-            group_z(nc.scalar.copy, G, 0, slice(0, TAIL_SPLIT))
+            group_z(nc.scalar.copy, G, 0)
             scale_pool(1, range(G, GROUPS))
             add_resid(last, 1)
             turn_z(last - 1)
             turn_pool(0)
             turn_pool(1)
-            empty_y(last - 2)
-            store_y(last - 2, 1)
             empty_z(last - 1)
             turn_z(last)
             turn_pool(G)
@@ -544,21 +561,25 @@ def tile_reglu_down_two_reads_s8_kernel(
             empty_pool(1)
             empty_pool(G)
             empty_z(last)
-            group_z(nc.vector.tensor_copy, G, 0, slice(TAIL_SPLIT, HALF))
-            quant_z(G - 1, 1)
+            empty_y(last - 2)
+            store_y(last - 2, 1)
+            group_z(nc.vector.tensor_copy, G, 1)
+            quant_z(G - 1, 3)
+            quant_z(G, 0)
             quant_zt(last - 1)
             project(last - 1)
-            quant_z(G, 0)
+            quant_z(G, 1)
             quant_pool(0)
-            quant_pool(1)
             group_z(nc.vector.tensor_copy, G, 2)
+            quant_pool(1)
+            group_z(nc.vector.tensor_copy, G, 3)
             quant_pool(G)
             for g in range(GROUPS):
                 gather(0, 0, range(g, g + 1))
                 gather(1, 0, range(g, g + 1))
-            group_z(nc.vector.tensor_copy, G, 3)
+            quant_z(G, 2)
             quant_zt(last)
-            quant_z(G, 1)
+            quant_z(G, 3)
             gather(0, 1, range(1))
             project(last)
             gather(0, 1, range(1, GROUPS))

@@ -33,9 +33,9 @@ BANKS = 8
 W_SPLIT = 320
 ALL = slice(0, F)
 LEFT, RIGHT = slice(0, F // 2), slice(F // 2, F)
-RELU_VECTOR, RELU_SCALAR = slice(0, 5 * F // 8), slice(5 * F // 8, F)
+RELU_VECTOR, RELU_SCALAR = slice(0, 13 * F // 16), slice(13 * F // 16, F)
 UP_SLOTS = 5
-BESIDE_ADDS = 192
+TAIL_SPLIT = 192
 RUN = 4
 
 
@@ -74,12 +74,11 @@ def tile_reglu_down_two_reads_s8_kernel(
         head_sc = keep.tile([P, HALVES, N], U8, name="head_sc", align_bytes=256)
         code_bytes = keep.tile([P, SLOT_TILES, M], U8, name="code_bytes", align_bytes=256)
         scale_row = keep.tile([P, M], F32, name="scale_row", align_bytes=256)
-        pool_bf = keep.tile([P, SLOT_TILES, M], BF16, name="pool_bf", align_bytes=256)
         ident = keep.tile([P, P], F32, name="ident", align_bytes=256)
 
         gates, ups, resids, relus, hs, hbanks, hts, hcs, hss = {}, {}, {}, {}, {}, {}, {}, {}, {}
         accs, zs, zbanks, zts, zcs, zss, ybanks, ys = {}, {}, {}, {}, {}, {}, {}, {}
-        wraws, wgs, zis, pbanks, pts, cbanks = {}, {}, {}, {}, {}, {}
+        wraws, wgs, zis, wides, pools, pbanks, pts, cbanks = {}, {}, {}, {}, {}, {}, {}, {}
 
 
         def load_gate(i, cols=ALL):
@@ -276,49 +275,48 @@ def tile_reglu_down_two_reads_s8_kernel(
             )
 
 
-        def z_chunk(G, c, tag="zi", bufs=4):
-            zis[G, c] = sb.tile([P, CHUNK, PACK], BF16, tag=tag, name="z_grouped", bufs=bufs, align_bytes=256)
-
         def group_z(copy, G, c, cols=slice(0, CHUNK)):
-            if (G, c) not in zis:
-                z_chunk(G, c)
+            h, c0 = divmod(c * CHUNK, HALF)
+            if (G, h) not in zis:
+                zis[G, h] = sb.tile([P, HALF, PACK], BF16, tag="zi", name="z_grouped", bufs=3, align_bytes=256)
             copy(
-                out=zis[G, c][:, cols, :].rearrange("p (c i) t -> p c t i", i=RUN),
+                out=zis[G, h][:, c0 + cols.start : c0 + cols.stop, :].rearrange("p (c i) t -> p c t i", i=RUN),
                 in_=zs[G][:, :, c * CHUNK + cols.start : c * CHUNK + cols.stop].rearrange(
                     "p t (c i) -> p c t i", i=RUN
                 ),
             )
 
-        def group_z_beside_adds(i, G, c):
-            z_chunk(G, c, "up%d" % (i % UP_SLOTS), 1)
-            nc.gpsimd.tensor_scalar(
-                out=zis[G, c][:, :BESIDE_ADDS, :],
-                in0=zs[G][:, :, c * CHUNK : c * CHUNK + BESIDE_ADDS].rearrange("p t c -> p c t"),
-                scalar1=1.0,
-                scalar2=0.0,
-                op0=MULT,
-                op1=ADD,
-            )
-            group_z(nc.scalar.copy, G, c, slice(BESIDE_ADDS, CHUNK))
-
-        def quant_z(G, c):
-            cols = slice(c * CHUNK, (c + 1) * CHUNK)
+        def quant_z(G, h):
+            cols = slice(h * HALF, (h + 1) * HALF)
             nc.vector.quantize_mx(
                 out=z_codes[:, G, cols].bitcast(FP8X4),
                 scales=z_scales[:, G, cols],
-                in_=zis[G, c][:].rearrange("p d t -> p (d t)"),
+                in_=zis[G, h][:].rearrange("p d t -> p (d t)"),
             )
 
-        def scale_pool(a, groups):
-            toks = slice(groups.start * K_PASS, groups.stop * K_PASS)
+        def scale_pool(a, G):
+            toks = slice(G * K_PASS, (G + 1) * K_PASS)
+            pools[a, G] = sb.tile([P, K_PASS], BF16, tag="pool", name="pool_bf", bufs=4, align_bytes=256)
             nc.vector.tensor_tensor(
-                out=pool_bf[:, a, toks], in0=code_bytes[:, a, toks].bitcast(FP8), in1=scale_row[:, toks], op=MULT
+                out=pools[a, G][:], in0=code_bytes[:, a, toks].bitcast(FP8), in1=scale_row[:, toks], op=MULT
+            )
+
+        def widen_pool(a, G):
+            wides[a, G] = sb.tile([P, K_PASS], BF16, tag="wide", name="pool_wide", bufs=2, align_bytes=256)
+            nc.scalar.copy(out=wides[a, G][:], in_=code_bytes[:, a, G * K_PASS : (G + 1) * K_PASS].bitcast(FP8))
+
+        def scale_pool_beside_adds(a, G, i):
+            pools[a, G] = sb.tile(
+                [P, K_PASS], BF16, tag="up%d" % (i % UP_SLOTS), name="pool_bf", bufs=1, align_bytes=256
+            )
+            nc.gpsimd.tensor_tensor(
+                out=pools[a, G][:], in0=wides[a, G][:], in1=scale_row[:, G * K_PASS : (G + 1) * K_PASS], op=MULT
             )
 
         def turn_pool(G):
             pbanks[G] = take_bank("pool_turned", G, [P, SLOT_TILES, 2, P])
             for a in range(SLOT_TILES):
-                words = pool_bf[:, a, G * K_PASS : (G + 1) * K_PASS].bitcast(F32)
+                words = pools[a, G][:].bitcast(F32)
                 for u in range(2):
                     nc.tensor.transpose(pbanks[G][:, a, u, :], words[:, u : K_PASS // 2 : 2], ident[:])
 
@@ -478,32 +476,28 @@ def tile_reglu_down_two_reads_s8_kernel(
             load_gate(7)
             load_up(7)
             load_resid(5)
-            relu_s(6, slice(13 * F // 16, F))
+            relu_s(6, RELU_SCALAR)
             last, G = TILES - 1, GROUPS - 1
 
             for a in range(4, last, 2):
-                load_gate(a + 4)
-                load_up(a + 4)
-                load_resid(a + 2)
-                load_gate(a + 5)
-                load_resid(a + 3)
-                load_up(a + 5)
+                for i in (a, a + 1):
+                    load_gate(i + 4)
+                    load_up(i + 4)
+                    load_resid(i + 2)
                 if a == 4:
                     load_pool()
                 turn_h(a)
                 turn_z(a - 2)
                 turn_h(a + 1)
                 add_resid(a - 1, 1)
-                relu_v(a + 2, RELU_VECTOR if a > 4 else slice(0, 13 * F // 16))
+                relu_v(a + 2, RELU_VECTOR if a <= 6 else ALL)
                 empty_h(a, 0)
                 empty_h(a, 1)
                 turn_z(a - 1)
                 quant_h(a, slice(0, 2))
                 if a >= 6:
-                    quant_z(*divmod(a - 6, PACK))
+                    quant_z(*divmod((a - 6) // 2, HALVES))
                 quant_h(a, slice(2, 4))
-                if a >= 6:
-                    quant_z(*divmod(a - 5, PACK))
                 project(a - 3)
                 empty_h(a + 1, 0)
                 empty_h(a + 1, 1)
@@ -511,32 +505,37 @@ def tile_reglu_down_two_reads_s8_kernel(
                 empty_z(a - 1)
                 down(a, 0)
                 down(a, 1)
-                if a == last - 1:
-                    scale_pool(0, range(1, 2))
-                    scale_pool(1, range(1, 2))
                 product(a + 2)
-                empty_y(a - 3)
-                relu_s(a + 3, RELU_SCALAR)
+                if a == last - 1:
+                    scale_pool(0, 1)
+                    scale_pool(1, 1)
                 quant_zt(a - 2)
                 project(a - 2)
                 quant_h(a + 1)
+                empty_y(a - 3)
                 add_resid(a, 0)
+                if a == 4:
+                    relu_s(a + 3, RELU_SCALAR)
                 group_z(nc.scalar.copy, *divmod(a - PACK, PACK))
+                if 6 <= a < last - 1:
+                    widen_pool((a - 6) // 2, 0)
                 empty_y(a - 2)
                 if a + 1 < last:
                     down(a + 1, 0)
                     down(a + 1, 1)
-                    relu_v(a + 3, RELU_VECTOR)
+                    relu_v(a + 3, RELU_VECTOR if a == 4 else ALL)
                     add_resid(a, 1)
-                    if a >= 6:
-                        scale_pool((a - 6) // 2, range(0, 1))
                     product(a + 3)
-                    group_z_beside_adds(a + 3, *divmod(a + 1 - PACK, PACK))
-                    relu_s(a + 4, RELU_SCALAR)
+                    if a >= 6:
+                        scale_pool_beside_adds((a - 6) // 2, 0, a + 3)
                     quant_zt(a - 1)
                     add_resid(a + 1, 0)
+                    group_z(nc.scalar.copy, *divmod(a + 1 - PACK, PACK))
+                    if a == 4:
+                        relu_s(a + 4, RELU_SCALAR)
                 if a >= 6:
                     store_y(a - 6, 2)
+
             down(last, 0)
             down(last, 1)
             store_y(last - 5, 2)
@@ -545,15 +544,16 @@ def tile_reglu_down_two_reads_s8_kernel(
             project(last - 2)
             add_resid(last - 1, 1)
             group_z(nc.scalar.copy, G - 1, 3)
-            scale_pool(0, range(G, GROUPS))
-            quant_z(G - 1, 2)
+            scale_pool(0, G)
             add_resid(last, 0)
-            group_z(nc.scalar.copy, G, 0)
-            scale_pool(1, range(G, GROUPS))
+            group_z(nc.scalar.copy, G, 0, slice(0, TAIL_SPLIT))
+            scale_pool(1, G)
             add_resid(last, 1)
             turn_z(last - 1)
             turn_pool(0)
             turn_pool(1)
+            empty_y(last - 2)
+            store_y(last - 2, 1)
             empty_z(last - 1)
             turn_z(last)
             turn_pool(G)
@@ -561,25 +561,21 @@ def tile_reglu_down_two_reads_s8_kernel(
             empty_pool(1)
             empty_pool(G)
             empty_z(last)
-            empty_y(last - 2)
-            store_y(last - 2, 1)
-            group_z(nc.vector.tensor_copy, G, 1)
-            quant_z(G - 1, 3)
-            quant_z(G, 0)
+            group_z(nc.vector.tensor_copy, G, 0, slice(TAIL_SPLIT, HALF))
+            quant_z(G - 1, 1)
             quant_zt(last - 1)
             project(last - 1)
-            quant_z(G, 1)
+            quant_z(G, 0)
             quant_pool(0)
-            group_z(nc.vector.tensor_copy, G, 2)
             quant_pool(1)
-            group_z(nc.vector.tensor_copy, G, 3)
+            group_z(nc.vector.tensor_copy, G, 2)
             quant_pool(G)
             for g in range(GROUPS):
                 gather(0, 0, range(g, g + 1))
                 gather(1, 0, range(g, g + 1))
-            quant_z(G, 2)
+            group_z(nc.vector.tensor_copy, G, 3)
             quant_zt(last)
-            quant_z(G, 3)
+            quant_z(G, 1)
             gather(0, 1, range(1))
             project(last)
             gather(0, 1, range(1, GROUPS))

@@ -512,6 +512,8 @@ def tile_reglu_down_two_reads_s8_kernel(
                 quant_zt(a - 2)
                 project(a - 2)
                 quant_h(a + 1)
+                if a >= 6:
+                    relu_v(a + 3, ALL)
                 empty_y(a - 3)
                 add_resid(a, 0)
                 if a == 4:
@@ -523,12 +525,15 @@ def tile_reglu_down_two_reads_s8_kernel(
                 if a + 1 < last:
                     down(a + 1, 0)
                     down(a + 1, 1)
-                    relu_v(a + 3, RELU_VECTOR if a == 4 else ALL)
-                    add_resid(a, 1)
+                    if a == 4:
+                        relu_v(a + 3, RELU_VECTOR)
+                        add_resid(a, 1)
                     product(a + 3)
                     if a >= 6:
                         scale_pool_beside_adds((a - 6) // 2, 0, a + 3)
                     quant_zt(a - 1)
+                    if a >= 6:
+                        add_resid(a, 1)
                     add_resid(a + 1, 0)
                     group_z(nc.scalar.copy, *divmod(a + 1 - PACK, PACK))
                     if a == 4:

@@ -36,6 +36,7 @@ LEFT, RIGHT = slice(0, F // 2), slice(F // 2, F)
 RELU_VECTOR, RELU_SCALAR = slice(0, 13 * F // 16), slice(13 * F // 16, F)
 UP_SLOTS = 5
 TAIL_SPLIT = 192
+BESIDE_ADDS = 192
 RUN = 4
 
 
@@ -286,6 +287,19 @@ def tile_reglu_down_two_reads_s8_kernel(
                 ),
             )
 
+        def group_z_beside_adds(G, h, i):
+            zis[G, h] = sb.tile(
+                [P, HALF, PACK], BF16, tag="up%d" % (i % UP_SLOTS), name="z_grouped", bufs=1, align_bytes=256
+            )
+            nc.gpsimd.tensor_scalar(
+                out=zis[G, h][:, :BESIDE_ADDS, :],
+                in0=zs[G][:, :, h * HALF : h * HALF + BESIDE_ADDS].rearrange("p t c -> p c t"),
+                scalar1=1.0,
+                scalar2=0.0,
+                op0=MULT,
+                op1=ADD,
+            )
+
         def quant_z(G, h):
             cols = slice(h * HALF, (h + 1) * HALF)
             nc.vector.quantize_mx(
@@ -310,7 +324,10 @@ def tile_reglu_down_two_reads_s8_kernel(
                 [P, K_PASS], BF16, tag="up%d" % (i % UP_SLOTS), name="pool_bf", bufs=1, align_bytes=256
             )
             nc.gpsimd.tensor_tensor(
-                out=pools[a, G][:], in0=wides[a, G][:], in1=scale_row[:, G * K_PASS : (G + 1) * K_PASS], op=MULT
+                out=pools[a, G][:].rearrange("p (u q e) -> p u q e", u=2, e=2),
+                in0=wides[a, G][:].rearrange("p (q u e) -> p u q e", u=2, e=2),
+                in1=scale_row[:, G * K_PASS : (G + 1) * K_PASS].rearrange("p (q u e) -> p u q e", u=2, e=2),
+                op=MULT,
             )
 
         def turn_pool(G):
@@ -318,7 +335,8 @@ def tile_reglu_down_two_reads_s8_kernel(
             for a in range(SLOT_TILES):
                 words = pools[a, G][:].bitcast(F32)
                 for u in range(2):
-                    nc.tensor.transpose(pbanks[G][:, a, u, :], words[:, u : K_PASS // 2 : 2], ident[:])
+                    picked = slice(u * P, (u + 1) * P) if G == 0 else slice(u, K_PASS // 2, 2)
+                    nc.tensor.transpose(pbanks[G][:, a, u, :], words[:, picked], ident[:])
 
         def empty_pool(G):
             pts[G] = sb.tile([P, SLOT_TILES, P, 2], F32, tag="pt", name="pool_grouped", bufs=3, align_bytes=256)
@@ -490,7 +508,7 @@ def tile_reglu_down_two_reads_s8_kernel(
                 turn_z(a - 2)
                 turn_h(a + 1)
                 add_resid(a - 1, 1)
-                relu_v(a + 2, RELU_VECTOR if a <= 6 else ALL)
+                relu_v(a + 2, RELU_VECTOR)
                 empty_h(a, 0)
                 empty_h(a, 1)
                 turn_z(a - 1)
@@ -512,31 +530,28 @@ def tile_reglu_down_two_reads_s8_kernel(
                 quant_zt(a - 2)
                 project(a - 2)
                 quant_h(a + 1)
-                if a >= 6:
-                    relu_v(a + 3, ALL)
+                relu_v(a + 3, RELU_VECTOR if a <= 6 else ALL)
                 empty_y(a - 3)
                 add_resid(a, 0)
-                if a == 4:
+                if a <= 6:
                     relu_s(a + 3, RELU_SCALAR)
-                group_z(nc.scalar.copy, *divmod(a - PACK, PACK))
+                group_z(nc.scalar.copy, *divmod(a - PACK, PACK), slice(BESIDE_ADDS if a == 6 else 0, CHUNK))
                 if 6 <= a < last - 1:
                     widen_pool((a - 6) // 2, 0)
                 empty_y(a - 2)
                 if a + 1 < last:
                     down(a + 1, 0)
                     down(a + 1, 1)
-                    if a == 4:
-                        relu_v(a + 3, RELU_VECTOR)
-                        add_resid(a, 1)
                     product(a + 3)
                     if a >= 6:
                         scale_pool_beside_adds((a - 6) // 2, 0, a + 3)
+                    else:
+                        group_z_beside_adds(0, 1, a + 3)
                     quant_zt(a - 1)
-                    if a >= 6:
-                        add_resid(a, 1)
+                    add_resid(a, 1)
                     add_resid(a + 1, 0)
                     group_z(nc.scalar.copy, *divmod(a + 1 - PACK, PACK))
-                    if a == 4:
+                    if a <= 6:
                         relu_s(a + 4, RELU_SCALAR)
                 if a >= 6:
                     store_y(a - 6, 2)

@@ -99,6 +99,11 @@ def tile_reglu_down_two_reads_s8_kernel(
                 resids[i] = sb.tile([P, D], BF16, tag="resid", name="resid_sb", bufs=5, align_bytes=256)
                 nc.sync.dma_start(out=resids[i][:], in_=resid_v[i // PACK][:, i % PACK, :])
 
+        def load_resid_pair(i):
+            pair = sb.tile([P, 2, D], BF16, tag="zi", name="resid_pair", bufs=3, align_bytes=256)
+            nc.sync.dma_start(out=pair[:], in_=resid_v[i // PACK][:, i % PACK : i % PACK + 2, :])
+            resids[i], resids[i + 1] = pair[:, 0, :], pair[:, 1, :]
+
         def load_w(g, h):
             wraws[g, h] = sb.tile([P, PACK, HALF], BF16, tag="wraw", name="w_raw", bufs=6, align_bytes=256)
             nc.sync.dma_start(out=wraws[g, h][:], in_=w_v[g][:, :, h * HALF : (h + 1) * HALF])
@@ -411,11 +416,11 @@ def tile_reglu_down_two_reads_s8_kernel(
             load_resid(1)
             load_gate(3)
             load_up(3)
-            load_gate(4)
-            load_up(4)
             load_head()
             load_head_scales()
-            load_resid(2)
+            load_gate(4)
+            load_up(4)
+            load_resid_pair(2)
             empty_h(0, 0)
             empty_h(0, 1)
             relu_v(1, ALL)
@@ -425,7 +430,6 @@ def tile_reglu_down_two_reads_s8_kernel(
             quant_h(0)
             load_gate(5)
             load_up(5)
-            load_resid(3)
             product(1)
             turn_h(1)
             quant_w(3, 0)

@@ -115,9 +115,15 @@ def tile_reglu_down_two_reads_s8_kernel(
             for q in range(PACK):
                 rows = slice(32 * q, 32 * q + 4)
                 nc.sync.dma_start(
-                    out=head_sc[rows, :, :].bitcast(I32),
+                    out=sc_loaded[rows, :, :].bitcast(I32),
                     in_=head_scales[:, 4 * q : 4 * q + 4, :].rearrange("g q n -> q g n").bitcast(I32),
                 )
+
+        def pass_on_head_scales():
+            nc.scalar.copy(
+                out=head_sc[:].rearrange("p g n -> p (g n)").bitcast(U32),
+                in_=sc_loaded[:].rearrange("p g n -> p (g n)").bitcast(U32),
+            )
 
         def load_pool():
             nc.sync.dma_start(out=scale_row[:], in_=pool_scale.rearrange("o k -> (o k)").partition_broadcast(P))
@@ -174,8 +180,9 @@ def tile_reglu_down_two_reads_s8_kernel(
 
         def turn_h(i):
             words = hs[i][:].bitcast(F32)
-            for b in range(2):
+            for b in (1, 0) if i == 4 else (0, 1):
                 hbanks[i, b] = take_bank("h_turned", (i, b), [P, 2, 2, P])
+            for b in range(2):
                 for gb in range(2):
                     for u in range(2):
                         w0 = u * (F // 4) + (2 * b + gb) * P
@@ -231,10 +238,14 @@ def tile_reglu_down_two_reads_s8_kernel(
             give_bank("z_acc", (i, h))
 
 
+        def book_z(i):
+            zbanks[i] = take_bank("z_turned", i, [P, HALVES, 2, P])
+
         def turn_z(i):
             G, t = divmod(i, PACK)
             words = zs[G][:, t, :].bitcast(F32)
-            zbanks[i] = take_bank("z_turned", i, [P, HALVES, 2, P])
+            if i not in zbanks:
+                book_z(i)
             for h in range(HALVES):
                 for u in range(2):
                     w0 = h * (HALF // 2) + u * P
@@ -335,8 +346,12 @@ def tile_reglu_down_two_reads_s8_kernel(
                 op=MULT,
             )
 
-        def turn_pool(G):
+        def book_pool(G):
             pbanks[G] = take_bank("pool_turned", G, [P, SLOT_TILES, 2, P])
+
+        def turn_pool(G):
+            if G not in pbanks:
+                book_pool(G)
             for a in range(SLOT_TILES):
                 words = pools[a, G][:].bitcast(F32)
                 for u in range(2):
@@ -383,7 +398,8 @@ def tile_reglu_down_two_reads_s8_kernel(
             )
 
         with tc.manual_schedule():
-            nc.vector.memset(head_sc[:].rearrange("p g n -> p (g n)").bitcast(I32), 0)
+            sc_loaded = sb.tile([P, HALVES, N], U8, tag="pool", name="head_sc_loaded", bufs=4, align_bytes=256)
+            nc.vector.memset(sc_loaded[:].rearrange("p g n -> p (g n)").bitcast(I32), 0)
             make_identity(nc, ident[:])
 
             load_w(0, 0)
@@ -471,6 +487,7 @@ def tile_reglu_down_two_reads_s8_kernel(
             turn_z(0)
             turn_h(3)
             turn_z(1)
+            pass_on_head_scales()
             empty_z(0)
             empty_h(3, 0)
             empty_h(3, 1)
@@ -508,6 +525,7 @@ def tile_reglu_down_two_reads_s8_kernel(
                     load_resid(i + 2)
                 if a == 4:
                     load_pool()
+                book_z(a - 2)
                 turn_h(a)
                 turn_z(a - 2)
                 turn_h(a + 1)
@@ -573,8 +591,10 @@ def tile_reglu_down_two_reads_s8_kernel(
             group_z(nc.scalar.copy, G, 0, slice(0, TAIL_SPLIT))
             scale_pool(1, G)
             add_resid(last, 1)
+            book_pool(0)
             turn_z(last - 1)
             turn_pool(0)
+            book_z(last)
             turn_pool(1)
             empty_y(last - 2)
             store_y(last - 2, 1)

@@ -27,6 +27,7 @@ F_PASSES = F // K_PASS
 HALF = 512
 HALVES = D // HALF
 CHUNK = HALF // 2
+PIECE = CHUNK // 2
 SLOT_TILES = R // P
 BANKS = 8
 
@@ -36,7 +37,7 @@ LEFT, RIGHT = slice(0, F // 2), slice(F // 2, F)
 RELU_VECTOR, RELU_SCALAR = slice(0, 13 * F // 16), slice(13 * F // 16, F)
 UP_SLOTS = 5
 TAIL_SPLIT = 192
-BESIDE_ADDS = 192
+BESIDE_ADDS = 96
 RUN = 4
 
 
@@ -292,36 +293,50 @@ def tile_reglu_down_two_reads_s8_kernel(
             )
 
 
-        def group_z(copy, G, c, cols=slice(0, CHUNK)):
-            h, c0 = divmod(c * CHUNK, HALF)
+        def grouped_z(G, h):
             if (G, h) not in zis:
                 zis[G, h] = sb.tile([P, HALF, PACK], BF16, tag="zi", name="z_grouped", bufs=3, align_bytes=256)
+            return zis[G, h]
+
+        def group_z_low(copy, G, cols):
             copy(
-                out=zis[G, h][:, c0 + cols.start : c0 + cols.stop, :].rearrange("p (c i) t -> p c t i", i=RUN),
-                in_=zs[G][:, :, c * CHUNK + cols.start : c * CHUNK + cols.stop].rearrange(
-                    "p t (c i) -> p c t i", i=RUN
-                ),
+                out=grouped_z(G, 0)[:, cols, :].rearrange("p (c i) t -> p c t i", i=RUN),
+                in_=zs[G][:, :, cols].rearrange("p t (c i) -> p c t i", i=RUN),
             )
 
-        def group_z_beside_adds(G, h, i):
-            zis[G, h] = sb.tile(
+        def chunk_views(G, k, cols):
+            return (
+                zis[G, 1][:].rearrange("p (k u c) t -> p k u c t", k=2, u=2)[:, k, :, cols, :],
+                zs[G][:, :, HALF:].rearrange("p t (u k c) -> p k u c t", k=2, u=2)[:, k, :, cols, :],
+            )
+
+        def group_z_high(copy, G, k, cols=slice(0, PIECE)):
+            grouped_z(G, 1)
+            out, in_ = chunk_views(G, k, cols)
+            copy(
+                out=out.rearrange("p u (c i) t -> p u c t i", i=RUN),
+                in_=in_.rearrange("p u (c i) t -> p u c t i", i=RUN),
+            )
+
+        def group_z(copy, G, c):
+            if c < 2:
+                group_z_low(copy, G, slice(c * CHUNK, (c + 1) * CHUNK))
+            else:
+                group_z_high(copy, G, c - 2)
+
+        def group_z_beside_adds(G, i):
+            zis[G, 1] = sb.tile(
                 [P, HALF, PACK], BF16, tag="up%d" % (i % UP_SLOTS), name="z_grouped", bufs=1, align_bytes=256
             )
-            nc.gpsimd.tensor_scalar(
-                out=zis[G, h][:, :BESIDE_ADDS, :],
-                in0=zs[G][:, :, h * HALF : h * HALF + BESIDE_ADDS].rearrange("p t c -> p c t"),
-                scalar1=1.0,
-                scalar2=0.0,
-                op0=MULT,
-                op1=ADD,
-            )
+            out, in_ = chunk_views(G, 0, slice(0, BESIDE_ADDS))
+            nc.gpsimd.tensor_scalar(out=out, in0=in_, scalar1=1.0, scalar2=0.0, op0=MULT, op1=ADD)
 
-        def quant_z(G, h):
-            cols = slice(h * HALF, (h + 1) * HALF)
+        def quant_z(G, h, part=slice(0, HALF)):
+            cols = slice(h * HALF + part.start, h * HALF + part.stop)
             nc.vector.quantize_mx(
                 out=z_codes[:, G, cols].bitcast(FP8X4),
                 scales=z_scales[:, G, cols],
-                in_=zis[G, h][:].rearrange("p d t -> p (d t)"),
+                in_=zis[G, h][:, part, :].rearrange("p d t -> p (d t)"),
             )
 
         def scale_pool(a, G):
@@ -370,14 +385,15 @@ def tile_reglu_down_two_reads_s8_kernel(
                 in_=pts[G][:].rearrange("p a r u -> p (a r u)").bitcast(BF16),
             )
 
-        def gather(a, h, groups):
-            if (a, h) not in cbanks:
-                cbanks[a, h] = take_bank("c_acc", (a, h), [P, HALF])
-            cols = slice(h * HALF, (h + 1) * HALF)
+        def gather(a, h, groups, part=slice(0, HALF)):
+            key = (a, h, part.start)
+            if key not in cbanks:
+                cbanks[key] = take_bank("c_acc", key, [P, part.stop - part.start])
+            cols = slice(h * HALF + part.start, h * HALF + part.stop)
             slots = slice(a * P, (a + 1) * P)
             for G in groups:
                 nc.tensor.matmul_mx(
-                    out=cbanks[a, h][:],
+                    out=cbanks[key][:],
                     lhsT=pool_codes[:, G, slots].bitcast(FP8X4),
                     lhsT_scale=pool_scales[:, G, slots],
                     rhs=z_codes[:, G, cols].bitcast(FP8X4),
@@ -386,15 +402,15 @@ def tile_reglu_down_two_reads_s8_kernel(
                     stop=(G == GROUPS - 1),
                 )
 
-        def store_c(copy, a, h, cols=slice(0, HALF)):
-            width = cols.stop - cols.start
-            c_sb = sb.tile([P, width], F32, tag="c", name="c_sb", bufs=5, align_bytes=256)
+        def store_c(copy, a, h, part=slice(0, HALF)):
+            width = part.stop - part.start
+            c_sb = keep.tile([P, width], F32, name="c_sb_%d_%d" % (a, h * HALF + part.start), align_bytes=256)
             copy(
                 out=c_sb[:].rearrange("p (q u e) -> p q u e", u=2, e=2),
-                in_=cbanks[a, h][:].rearrange("p (u q e) -> p q u e", u=2, e=2)[:, cols.start // 4 : cols.stop // 4],
+                in_=cbanks[a, h, part.start][:].rearrange("p (u q e) -> p q u e", u=2, e=2),
             )
             nc.sync.dma_start(
-                out=out_c[a * P : (a + 1) * P, h * HALF + cols.start : h * HALF + cols.stop], in_=c_sb[:]
+                out=out_c[a * P : (a + 1) * P, h * HALF + part.start : h * HALF + part.stop], in_=c_sb[:]
             )
 
         with tc.manual_schedule():
@@ -557,7 +573,10 @@ def tile_reglu_down_two_reads_s8_kernel(
                 add_resid(a, 0)
                 if a <= 6:
                     relu_s(a + 3, RELU_SCALAR)
-                group_z(nc.scalar.copy, *divmod(a - PACK, PACK), slice(BESIDE_ADDS if a == 6 else 0, CHUNK))
+                if a == 6:
+                    group_z_high(nc.scalar.copy, 0, 0, slice(BESIDE_ADDS, PIECE))
+                else:
+                    group_z(nc.scalar.copy, *divmod(a - PACK, PACK))
                 if 6 <= a < last - 1:
                     widen_pool((a - 6) // 2, 0)
                 empty_y(a - 2)
@@ -568,7 +587,7 @@ def tile_reglu_down_two_reads_s8_kernel(
                     if a >= 6:
                         scale_pool_beside_adds((a - 6) // 2, 0, a + 3)
                     else:
-                        group_z_beside_adds(0, 1, a + 3)
+                        group_z_beside_adds(0, a + 3)
                     quant_zt(a - 1)
                     add_resid(a, 1)
                     add_resid(a + 1, 0)
@@ -588,7 +607,7 @@ def tile_reglu_down_two_reads_s8_kernel(
             group_z(nc.scalar.copy, G - 1, 3)
             scale_pool(0, G)
             add_resid(last, 0)
-            group_z(nc.scalar.copy, G, 0, slice(0, TAIL_SPLIT))
+            group_z_low(nc.scalar.copy, G, slice(0, TAIL_SPLIT))
             scale_pool(1, G)
             add_resid(last, 1)
             book_pool(0)
@@ -605,31 +624,38 @@ def tile_reglu_down_two_reads_s8_kernel(
             empty_pool(1)
             empty_pool(G)
             empty_z(last)
-            group_z(nc.vector.tensor_copy, G, 0, slice(TAIL_SPLIT, HALF))
+            group_z_low(nc.vector.tensor_copy, G, slice(TAIL_SPLIT, HALF))
             quant_z(G - 1, 1)
             quant_zt(last - 1)
             project(last - 1)
             quant_z(G, 0)
             quant_pool(0)
             quant_pool(1)
-            group_z(nc.vector.tensor_copy, G, 2)
             quant_pool(G)
-            for g in range(GROUPS):
-                gather(0, 0, range(g, g + 1))
-                gather(1, 0, range(g, g + 1))
-            group_z(nc.vector.tensor_copy, G, 3)
+            group_z(nc.vector.tensor_copy, G, 2)
             quant_zt(last)
-            quant_z(G, 1)
-            gather(0, 1, range(1))
+            group_z(nc.vector.tensor_copy, G, 3)
+            low, high = slice(0, CHUNK), slice(CHUNK, HALF)
+            quant_z(G, 1, low)
+            quant_z(G, 1, high)
+            gather(0, 0, range(2))
+            gather(1, 0, range(1))
+            gather(0, 0, range(2, 3))
+            gather(1, 0, range(1, 3))
             project(last)
-            gather(0, 1, range(1, GROUPS))
-            gather(1, 1, range(GROUPS))
+            gather(0, 1, range(G), low)
+            gather(1, 1, range(G), low)
+            gather(0, 1, range(G, GROUPS), low)
+            gather(1, 1, range(G, GROUPS), low)
+            gather(0, 1, range(GROUPS), high)
+            gather(1, 1, range(GROUPS), high)
             empty_y(last - 1)
             store_y(last - 1, 1)
             store_c(nc.scalar.copy, 0, 0)
             store_c(nc.scalar.copy, 1, 0)
             empty_y(last)
             store_y(last, 1)
-            store_c(nc.vector.tensor_copy, 0, 1)
-            for cols in (slice(0, CHUNK), slice(CHUNK, HALF)):
-                store_c(nc.scalar.copy, 1, 1, cols)
+            store_c(nc.vector.tensor_copy, 0, 1, low)
+            store_c(nc.scalar.copy, 1, 1, low)
+            store_c(nc.vector.tensor_copy, 0, 1, high)
+            store_c(nc.scalar.copy, 1, 1, high)

from contextlib import ExitStack

import concourse.mybir as mybir
from concourse.masks import make_identity

M, F, D, N, R = 1536, 2048, 1024, 512, 256
FLOPS = 2 * M * F * D + 2 * M * D * N + 2 * R * M * D

F32 = mybir.dt.float32
BF16 = mybir.dt.bfloat16
I32 = mybir.dt.int32
U32 = mybir.dt.uint32
U8 = mybir.dt.uint8
FP8 = mybir.dt.float8_e4m3fn
FP8X4 = mybir.dt.float8_e4m3fn_x4
FP4X4 = mybir.dt.float4_e2m1fn_x4
ADD = mybir.AluOpType.add
MULT = mybir.AluOpType.mult
RELU = mybir.ActivationFunctionType.Relu

P = 128
PACK = 4
K_PASS = P * PACK
TILES = M // P
GROUPS = M // K_PASS
F_PASSES = F // K_PASS
HALF = 512
HALVES = D // HALF
CHUNK = HALF // 2
PIECE = CHUNK // 2
SLOT_TILES = R // P
BANKS = 8

W_SPLIT = 320
ALL = slice(0, F)
LEFT, RIGHT = slice(0, F // 2), slice(F // 2, F)
RELU_VECTOR, RELU_SCALAR = slice(0, 13 * F // 16), slice(13 * F // 16, F)
UP_SLOTS = 5
TAIL_SPLIT = 192
BESIDE_ADDS = 96
RUN = 4


def tile_reglu_down_two_reads_s8_kernel(
    tc, gate, up, w_down, resid, head_words, head_scales, pool_bytes, pool_scale, out_y, out_c
):
    nc = tc.nc

    gate_v = gate.rearrange("(g p t) f -> g p t f", p=P, t=PACK)
    up_v = up.rearrange("(g p t) f -> g p t f", p=P, t=PACK)
    resid_v = resid.rearrange("(g p t) d -> g p t d", p=P, t=PACK)
    y_v = out_y.rearrange("(g p t) n -> g p t n", p=P, t=PACK)
    w_v = w_down.rearrange("(g p j) d -> g p j d", p=P, j=PACK)

    with ExitStack() as ctx:
        keep = ctx.enter_context(tc.tile_pool(name="keep", bufs=1))
        sb = ctx.enter_context(tc.tile_pool(name="sb", bufs=2))
        psum = ctx.enter_context(tc.psum_pool(name="psum", bufs=1))
        free_banks = list(range(BANKS))
        bank_of = {}

        def take_bank(name, key, shape):
            bank_of[name, key] = free_banks.pop(0)
            return psum.tile(shape, F32, tag="bank%d" % bank_of[name, key], name=name)

        def give_bank(name, key):
            free_banks.append(bank_of[name, key])

        w_codes = keep.tile([P, F_PASSES, D], U32, name="w_codes", align_bytes=256)
        w_scales = keep.tile([P, F_PASSES, D], U8, name="w_scales", align_bytes=256)
        z_codes = keep.tile([P, GROUPS, D], U32, name="z_codes", align_bytes=256)
        z_scales = keep.tile([P, GROUPS, D], U8, name="z_scales", align_bytes=256)
        pool_codes = keep.tile([P, GROUPS, R], U32, name="pool_codes", align_bytes=256)
        pool_scales = keep.tile([P, GROUPS, R], U8, name="pool_scales", align_bytes=256)
        head_sb = keep.tile([P, HALVES, 2 * N], U8, name="head_sb", align_bytes=256)
        head_sc = keep.tile([P, HALVES, N], U8, name="head_sc", align_bytes=256)
        code_bytes = keep.tile([P, SLOT_TILES, M], U8, name="code_bytes", align_bytes=256)
        scale_row = keep.tile([P, M], F32, name="scale_row", align_bytes=256)
        ident = keep.tile([P, P], F32, name="ident", align_bytes=256)

        gates, ups, resids, relus, hs, hbanks, hts, hcs, hss = {}, {}, {}, {}, {}, {}, {}, {}, {}
        accs, zs, zbanks, zts, zcs, zss, ybanks, ys = {}, {}, {}, {}, {}, {}, {}, {}
        wraws, wgs, zis, wides, pools, pbanks, pts, cbanks = {}, {}, {}, {}, {}, {}, {}, {}


        def load_gate(i, cols=ALL):
            if i < TILES:
                if i not in gates:
                    gates[i] = sb.tile([P, F], BF16, tag="gate", name="gate_sb", bufs=5, align_bytes=256)
                nc.sync.dma_start(out=gates[i][:, cols], in_=gate_v[i // PACK][:, i % PACK, cols])

        def load_up(i, cols=ALL):
            if i < TILES:
                if i not in ups:
                    ups[i] = sb.tile([P, F], BF16, tag="up%d" % (i % UP_SLOTS), name="up_sb", bufs=1, align_bytes=256)
                nc.sync.dma_start(out=ups[i][:, cols], in_=up_v[i // PACK][:, i % PACK, cols])

        def load_resid(i):
            if i < TILES:
                resids[i] = sb.tile([P, D], BF16, tag="resid", name="resid_sb", bufs=5, align_bytes=256)
                nc.sync.dma_start(out=resids[i][:], in_=resid_v[i // PACK][:, i % PACK, :])

        def load_resid_pair(i):
            pair = sb.tile([P, 2, D], BF16, tag="zi", name="resid_pair", bufs=3, align_bytes=256)
            nc.sync.dma_start(out=pair[:], in_=resid_v[i // PACK][:, i % PACK : i % PACK + 2, :])
            resids[i], resids[i + 1] = pair[:, 0, :], pair[:, 1, :]

        def load_w(g, h):
            wraws[g, h] = sb.tile([P, PACK, HALF], BF16, tag="wraw", name="w_raw", bufs=6, align_bytes=256)
            nc.sync.dma_start(out=wraws[g, h][:], in_=w_v[g][:, :, h * HALF : (h + 1) * HALF])

        def load_head():
            nc.sync.dma_start(out=head_sb[:], in_=head_words.rearrange("g p b -> p g b"))

        def load_head_scales():
            for q in range(PACK):
                rows = slice(32 * q, 32 * q + 4)
                nc.sync.dma_start(
                    out=sc_loaded[rows, :, :].bitcast(I32),
                    in_=head_scales[:, 4 * q : 4 * q + 4, :].rearrange("g q n -> q g n").bitcast(I32),
                )

        def pass_on_head_scales():
            nc.scalar.copy(
                out=head_sc[:].rearrange("p g n -> p (g n)").bitcast(U32),
                in_=sc_loaded[:].rearrange("p g n -> p (g n)").bitcast(U32),
            )

        def load_pool():
            nc.sync.dma_start(out=scale_row[:], in_=pool_scale.rearrange("o k -> (o k)").partition_broadcast(P))
            nc.sync.dma_start(out=code_bytes[:], in_=pool_bytes.rearrange("(a p) m -> p a m", p=P))


        def group_w(copy, g, h, cols):
            if (g, h) not in wgs:
                wgs[g, h] = sb.tile([P, HALF, PACK], BF16, tag="wg", name="w_grouped", bufs=3, align_bytes=256)
            copy(
                out=wgs[g, h][:, cols, :].rearrange("p (c i) j -> p c j i", i=RUN),
                in_=wraws[g, h][:, :, cols].rearrange("p j (c i) -> p c j i", i=RUN),
            )

        def group_w_s(g, h, split=W_SPLIT):
            group_w(nc.scalar.copy, g, h, slice(0, split))

        def group_w_v(g, h, split=W_SPLIT):
            group_w(nc.vector.tensor_copy, g, h, slice(split, HALF))

        def quant_w(g, h):
            cols = slice(h * HALF, (h + 1) * HALF)
            nc.vector.quantize_mx(
                out=w_codes[:, g, cols].bitcast(FP8X4),
                scales=w_scales[:, g, cols],
                in_=wgs[g, h][:].rearrange("p w j -> p (w j)"),
            )


        def relu_tile(i):
            if i not in relus:
                relus[i] = sb.tile([P, F], BF16, tag="relu", name="relu_sb", bufs=2, align_bytes=256)
            return relus[i]

        def relu_v(i, cols):
            if i < TILES:
                nc.vector.tensor_scalar_max(relu_tile(i)[:, cols], gates[i][:, cols], 0.0)

        def relu_s(i, cols):
            if i < TILES:
                nc.scalar.activation(relu_tile(i)[:, cols], gates[i][:, cols], func=RELU)

        def product(i, cols=ALL):
            if i < TILES:
                if i not in hs:
                    hs[i] = sb.tile([P, F], BF16, tag="h", name="h_sb", bufs=2, align_bytes=256)
                quads = slice(cols.start // 4, cols.stop // 4)
                nc.vector.tensor_tensor(
                    out=hs[i][:].rearrange("p (u q e) -> p u q e", u=2, e=2)[:, :, quads, :],
                    in0=relus[i][:, cols].rearrange("p (q u e) -> p u q e", u=2, e=2),
                    in1=ups[i][:, cols].rearrange("p (q u e) -> p u q e", u=2, e=2),
                    op=MULT,
                )

        def turn_h(i):
            words = hs[i][:].bitcast(F32)
            for b in (1, 0) if i == 4 else (0, 1):
                hbanks[i, b] = take_bank("h_turned", (i, b), [P, 2, 2, P])
            for b in range(2):
                for gb in range(2):
                    for u in range(2):
                        w0 = u * (F // 4) + (2 * b + gb) * P
                        nc.tensor.transpose(hbanks[i, b][:, gb, u, :], words[:, w0 : w0 + P], ident[:])

        def empty_h(i, b):
            if i not in hts:
                hts[i] = sb.tile([P, F_PASSES, P, 2], F32, tag="ht", name="h_grouped", bufs=2, align_bytes=256)
            nc.scalar.copy(
                out=hts[i][:, 2 * b : 2 * b + 2, :, :], in_=hbanks[i, b][:].rearrange("p g u m -> p g m u")
            )
            give_bank("h_turned", (i, b))

        def quant_h(i, passes=slice(0, F_PASSES)):
            if i not in hcs:
                hcs[i] = sb.tile([P, F_PASSES * P], U32, tag="hc", name="h_codes", bufs=4, align_bytes=256)
                hss[i] = sb.tile([P, F_PASSES * P], U8, tag="hs", name="h_scales", bufs=4, align_bytes=256)
            toks = slice(passes.start * P, passes.stop * P)
            nc.vector.quantize_mx(
                out=hcs[i][:, toks].bitcast(FP8X4),
                scales=hss[i][:, toks],
                in_=hts[i][:, passes, :, :].rearrange("p g m u -> p (g m u)").bitcast(BF16),
            )


        def down(i, h, passes=range(F_PASSES)):
            if (i, h) not in accs:
                accs[i, h] = take_bank("z_acc", (i, h), [P, HALF])
            cols = slice(h * HALF, (h + 1) * HALF)
            for g in passes:
                toks = slice(g * P, (g + 1) * P)
                nc.tensor.matmul_mx(
                    out=accs[i, h][:],
                    lhsT=hcs[i][:, toks].bitcast(FP8X4),
                    lhsT_scale=hss[i][:, toks],
                    rhs=w_codes[:, g, cols].bitcast(FP8X4),
                    rhs_scale=w_scales[:, g, cols],
                    start=(g == 0),
                    stop=(g == F_PASSES - 1),
                )

        def add_resid(i, h):
            G, t = divmod(i, PACK)
            if G not in zs:
                zs[G] = sb.tile([P, PACK, D], BF16, tag="z", name="z_sb", bufs=2, align_bytes=256)
            cols = slice(h * HALF, (h + 1) * HALF)
            nc.vector.tensor_tensor(
                out=zs[G][:, t, cols].rearrange("p (u q e) -> p u q e", u=2, e=2),
                in0=accs[i, h][:].rearrange("p (q u e) -> p u q e", u=2, e=2),
                in1=resids[i][:, cols].rearrange("p (q u e) -> p u q e", u=2, e=2),
                op=ADD,
            )
            give_bank("z_acc", (i, h))


        def book_z(i):
            zbanks[i] = take_bank("z_turned", i, [P, HALVES, 2, P])

        def turn_z(i):
            G, t = divmod(i, PACK)
            words = zs[G][:, t, :].bitcast(F32)
            if i not in zbanks:
                book_z(i)
            for h in range(HALVES):
                for u in range(2):
                    w0 = h * (HALF // 2) + u * P
                    nc.tensor.transpose(zbanks[i][:, h, u, :], words[:, w0 : w0 + P], ident[:])

        def empty_z(i):
            zts[i] = sb.tile([P, HALVES, P, 2], F32, tag="zt", name="zt_grouped", bufs=3, align_bytes=256)
            nc.scalar.copy(out=zts[i][:], in_=zbanks[i][:].rearrange("p h u m -> p h m u"))
            give_bank("z_turned", i)

        def quant_zt(i):
            zcs[i] = sb.tile([P, HALVES * P], U32, tag="ztc", name="zt_codes", bufs=3, align_bytes=256)
            zss[i] = sb.tile([P, HALVES * P], U8, tag="zts", name="zt_scales", bufs=3, align_bytes=256)
            nc.vector.quantize_mx(
                out=zcs[i][:].bitcast(FP8X4),
                scales=zss[i][:],
                in_=zts[i][:].rearrange("p h m u -> p (h m u)").bitcast(BF16),
            )

        def project(i):
            ybanks[i] = take_bank("y_acc", i, [P, N])
            for h in range(HALVES):
                toks = slice(h * P, (h + 1) * P)
                nc.tensor.matmul_mx(
                    out=ybanks[i][:],
                    lhsT=zcs[i][:, toks].bitcast(FP8X4),
                    lhsT_scale=zss[i][:, toks],
                    rhs=head_sb[:, h, :].bitcast(FP4X4),
                    rhs_scale=head_sc[:, h, :],
                    start=(h == 0),
                    stop=(h == HALVES - 1),
                )

        def empty_y(i):
            if i // 2 not in ys:
                ys[i // 2] = sb.tile([P, 2, N], F32, tag="wraw", name="y_sb", bufs=6, align_bytes=256)
            nc.scalar.copy(out=ys[i // 2][:, i % 2, :], in_=ybanks[i][:])
            give_bank("y_acc", i)

        def store_y(first, count):
            t = first % PACK
            nc.sync.dma_start(
                out=y_v[first // PACK][:, t : t + count, :], in_=ys[first // 2][:, first % 2 : first % 2 + count, :]
            )


        def grouped_z(G, h):
            if (G, h) not in zis:
                zis[G, h] = sb.tile([P, HALF, PACK], BF16, tag="zi", name="z_grouped", bufs=3, align_bytes=256)
            return zis[G, h]

        def group_z_low(copy, G, cols):
            copy(
                out=grouped_z(G, 0)[:, cols, :].rearrange("p (c i) t -> p c t i", i=RUN),
                in_=zs[G][:, :, cols].rearrange("p t (c i) -> p c t i", i=RUN),
            )

        def chunk_views(G, k, cols):
            return (
                zis[G, 1][:].rearrange("p (k u c) t -> p k u c t", k=2, u=2)[:, k, :, cols, :],
                zs[G][:, :, HALF:].rearrange("p t (u k c) -> p k u c t", k=2, u=2)[:, k, :, cols, :],
            )

        def group_z_high(copy, G, k, cols=slice(0, PIECE)):
            grouped_z(G, 1)
            out, in_ = chunk_views(G, k, cols)
            copy(
                out=out.rearrange("p u (c i) t -> p u c t i", i=RUN),
                in_=in_.rearrange("p u (c i) t -> p u c t i", i=RUN),
            )

        def group_z(copy, G, c):
            if c < 2:
                group_z_low(copy, G, slice(c * CHUNK, (c + 1) * CHUNK))
            else:
                group_z_high(copy, G, c - 2)

        def group_z_beside_adds(G, i):
            zis[G, 1] = sb.tile(
                [P, HALF, PACK], BF16, tag="up%d" % (i % UP_SLOTS), name="z_grouped", bufs=1, align_bytes=256
            )
            out, in_ = chunk_views(G, 0, slice(0, BESIDE_ADDS))
            nc.gpsimd.tensor_scalar(out=out, in0=in_, scalar1=1.0, scalar2=0.0, op0=MULT, op1=ADD)

        def quant_z(G, h, part=slice(0, HALF)):
            cols = slice(h * HALF + part.start, h * HALF + part.stop)
            nc.vector.quantize_mx(
                out=z_codes[:, G, cols].bitcast(FP8X4),
                scales=z_scales[:, G, cols],
                in_=zis[G, h][:, part, :].rearrange("p d t -> p (d t)"),
            )

        def scale_pool(a, G):
            toks = slice(G * K_PASS, (G + 1) * K_PASS)
            pools[a, G] = sb.tile([P, K_PASS], BF16, tag="pool", name="pool_bf", bufs=4, align_bytes=256)
            nc.vector.tensor_tensor(
                out=pools[a, G][:], in0=code_bytes[:, a, toks].bitcast(FP8), in1=scale_row[:, toks], op=MULT
            )

        def widen_pool(a, G):
            wides[a, G] = sb.tile([P, K_PASS], BF16, tag="wide", name="pool_wide", bufs=2, align_bytes=256)
            nc.scalar.copy(out=wides[a, G][:], in_=code_bytes[:, a, G * K_PASS : (G + 1) * K_PASS].bitcast(FP8))

        def scale_pool_beside_adds(a, G, i):
            pools[a, G] = sb.tile(
                [P, K_PASS], BF16, tag="up%d" % (i % UP_SLOTS), name="pool_bf", bufs=1, align_bytes=256
            )
            nc.gpsimd.tensor_tensor(
                out=pools[a, G][:].rearrange("p (u q e) -> p u q e", u=2, e=2),
                in0=wides[a, G][:].rearrange("p (q u e) -> p u q e", u=2, e=2),
                in1=scale_row[:, G * K_PASS : (G + 1) * K_PASS].rearrange("p (q u e) -> p u q e", u=2, e=2),
                op=MULT,
            )

        def book_pool(G):
            pbanks[G] = take_bank("pool_turned", G, [P, SLOT_TILES, 2, P])

        def turn_pool(G):
            if G not in pbanks:
                book_pool(G)
            for a in range(SLOT_TILES):
                words = pools[a, G][:].bitcast(F32)
                for u in range(2):
                    picked = slice(u * P, (u + 1) * P) if G == 0 else slice(u, K_PASS // 2, 2)
                    nc.tensor.transpose(pbanks[G][:, a, u, :], words[:, picked], ident[:])

        def empty_pool(G):
            pts[G] = sb.tile([P, SLOT_TILES, P, 2], F32, tag="pt", name="pool_grouped", bufs=3, align_bytes=256)
            nc.scalar.copy(out=pts[G][:], in_=pbanks[G][:].rearrange("p a u r -> p a r u"))
            give_bank("pool_turned", G)

        def quant_pool(G):
            nc.vector.quantize_mx(
                out=pool_codes[:, G, :].bitcast(FP8X4),
                scales=pool_scales[:, G, :],
                in_=pts[G][:].rearrange("p a r u -> p (a r u)").bitcast(BF16),
            )

        def gather(a, h, groups, part=slice(0, HALF)):
            key = (a, h, part.start)
            if key not in cbanks:
                cbanks[key] = take_bank("c_acc", key, [P, part.stop - part.start])
            cols = slice(h * HALF + part.start, h * HALF + part.stop)
            slots = slice(a * P, (a + 1) * P)
            for G in groups:
                nc.tensor.matmul_mx(
                    out=cbanks[key][:],
                    lhsT=pool_codes[:, G, slots].bitcast(FP8X4),
                    lhsT_scale=pool_scales[:, G, slots],
                    rhs=z_codes[:, G, cols].bitcast(FP8X4),
                    rhs_scale=z_scales[:, G, cols],
                    start=(G == 0),
                    stop=(G == GROUPS - 1),
                )

        def store_c(copy, a, h, part=slice(0, HALF)):
            width = part.stop - part.start
            c_sb = keep.tile([P, width], F32, name="c_sb_%d_%d" % (a, h * HALF + part.start), align_bytes=256)
            copy(
                out=c_sb[:].rearrange("p (q u e) -> p q u e", u=2, e=2),
                in_=cbanks[a, h, part.start][:].rearrange("p (u q e) -> p q u e", u=2, e=2),
            )
            nc.sync.dma_start(
                out=out_c[a * P : (a + 1) * P, h * HALF + part.start : h * HALF + part.stop], in_=c_sb[:]
            )

        with tc.manual_schedule():
            sc_loaded = sb.tile([P, HALVES, N], U8, tag="pool", name="head_sc_loaded", bufs=4, align_bytes=256)
            nc.vector.memset(sc_loaded[:].rearrange("p g n -> p (g n)").bitcast(I32), 0)
            make_identity(nc, ident[:])

            load_w(0, 0)
            load_gate(0)
            load_w(1, 0)
            load_up(0)
            load_w(2, 0)
            load_gate(1)
            load_w(3, 0)
            load_up(1)
            load_w(0, 1)
            load_gate(2)
            load_w(1, 1)
            load_up(2)

            group_w_s(0, 0)
            group_w_v(0, 0)
            relu_v(0, ALL)
            quant_w(0, 0)
            group_w_s(1, 0)
            group_w_v(1, 0)
            load_w(2, 1)
            product(0)
            turn_h(0)
            quant_w(1, 0)
            group_w_s(2, 0)
            group_w_v(2, 0)
            load_w(3, 1)
            load_resid(0)
            load_resid(1)
            load_gate(3)
            load_up(3)
            load_head()
            load_head_scales()
            load_gate(4)
            load_up(4)
            load_resid_pair(2)
            empty_h(0, 0)
            empty_h(0, 1)
            relu_v(1, ALL)
            quant_w(2, 0)
            group_w_s(3, 0)
            group_w_v(3, 0)
            quant_h(0)
            load_gate(5)
            load_up(5)
            product(1)
            turn_h(1)
            quant_w(3, 0)
            down(0, 0)
            group_w_s(0, 1)
            group_w_v(0, 1)
            empty_h(1, 0)
            empty_h(1, 1)
            relu_v(2, ALL)
            quant_w(0, 1)
            group_w_s(1, 1)
            group_w_v(1, 1)
            quant_h(1)
            down(1, 0)
            product(2)
            turn_h(2)
            quant_w(1, 1)
            down(0, 1, range(0, 2))
            down(1, 1, range(0, 2))
            group_w_s(2, 1, 192)
            group_w_v(2, 1, 192)
            group_w_s(3, 1, 192)
            group_w_v(3, 1, 192)
            empty_h(2, 0)
            empty_h(2, 1)
            quant_w(2, 1)
            quant_w(3, 1)
            down(0, 1, range(2, 4))
            down(1, 1, range(2, 4))
            add_resid(0, 0)
            quant_h(2)
            down(2, 0)
            relu_s(3, RIGHT)
            relu_v(3, LEFT)
            add_resid(0, 1)
            product(3)
            add_resid(1, 0)
            add_resid(1, 1)
            turn_z(0)
            turn_h(3)
            turn_z(1)
            pass_on_head_scales()
            empty_z(0)
            empty_h(3, 0)
            empty_h(3, 1)
            empty_z(1)
            down(2, 1)
            relu_v(4, ALL)
            quant_zt(0)
            project(0)
            product(4, LEFT)
            quant_h(3)
            product(4, RIGHT)
            down(3, 0)
            down(3, 1)
            add_resid(2, 0)
            relu_s(5, RIGHT)
            empty_y(0)
            relu_v(5, LEFT)
            add_resid(2, 1)
            quant_zt(1)
            product(5)
            add_resid(3, 0)
            load_gate(6)
            load_up(6)
            load_resid(4)
            load_gate(7)
            load_up(7)
            load_resid(5)
            relu_s(6, RELU_SCALAR)
            last, G = TILES - 1, GROUPS - 1

            for a in range(4, last, 2):
                for i in (a, a + 1):
                    load_gate(i + 4)
                    load_up(i + 4)
                    load_resid(i + 2)
                if a == 4:
                    load_pool()
                book_z(a - 2)
                turn_h(a)
                turn_z(a - 2)
                turn_h(a + 1)
                add_resid(a - 1, 1)
                relu_v(a + 2, RELU_VECTOR)
                empty_h(a, 0)
                empty_h(a, 1)
                turn_z(a - 1)
                quant_h(a, slice(0, 2))
                if a >= 6:
                    quant_z(*divmod((a - 6) // 2, HALVES))
                quant_h(a, slice(2, 4))
                project(a - 3)
                empty_h(a + 1, 0)
                empty_h(a + 1, 1)
                empty_z(a - 2)
                empty_z(a - 1)
                down(a, 0)
                down(a, 1)
                product(a + 2)
                if a == last - 1:
                    scale_pool(0, 1)
                    scale_pool(1, 1)
                quant_zt(a - 2)
                project(a - 2)
                quant_h(a + 1)
                relu_v(a + 3, RELU_VECTOR if a <= 6 else ALL)
                empty_y(a - 3)
                add_resid(a, 0)
                if a <= 6:
                    relu_s(a + 3, RELU_SCALAR)
                if a == 6:
                    group_z_high(nc.scalar.copy, 0, 0, slice(BESIDE_ADDS, PIECE))
                else:
                    group_z(nc.scalar.copy, *divmod(a - PACK, PACK))
                if 6 <= a < last - 1:
                    widen_pool((a - 6) // 2, 0)
                empty_y(a - 2)
                if a + 1 < last:
                    down(a + 1, 0)
                    down(a + 1, 1)
                    product(a + 3)
                    if a >= 6:
                        scale_pool_beside_adds((a - 6) // 2, 0, a + 3)
                    else:
                        group_z_beside_adds(0, a + 3)
                    quant_zt(a - 1)
                    add_resid(a, 1)
                    add_resid(a + 1, 0)
                    group_z(nc.scalar.copy, *divmod(a + 1 - PACK, PACK))
                    if a <= 6:
                        relu_s(a + 4, RELU_SCALAR)
                if a >= 6:
                    store_y(a - 6, 2)

            down(last, 0)
            down(last, 1)
            store_y(last - 5, 2)
            store_y(last - 3, 1)
            quant_zt(last - 2)
            project(last - 2)
            add_resid(last - 1, 1)
            group_z(nc.scalar.copy, G - 1, 3)
            scale_pool(0, G)
            add_resid(last, 0)
            group_z_low(nc.scalar.copy, G, slice(0, TAIL_SPLIT))
            scale_pool(1, G)
            add_resid(last, 1)
            book_pool(0)
            turn_z(last - 1)
            turn_pool(0)
            book_z(last)
            turn_pool(1)
            empty_y(last - 2)
            store_y(last - 2, 1)
            empty_z(last - 1)
            turn_z(last)
            turn_pool(G)
            empty_pool(0)
            empty_pool(1)
            empty_pool(G)
            empty_z(last)
            group_z_low(nc.vector.tensor_copy, G, slice(TAIL_SPLIT, HALF))
            quant_z(G - 1, 1)
            quant_zt(last - 1)
            project(last - 1)
            quant_z(G, 0)
            quant_pool(0)
            quant_pool(1)
            quant_pool(G)
            group_z(nc.vector.tensor_copy, G, 2)
            quant_zt(last)
            group_z(nc.vector.tensor_copy, G, 3)
            low, high = slice(0, CHUNK), slice(CHUNK, HALF)
            quant_z(G, 1, low)
            quant_z(G, 1, high)
            gather(0, 0, range(2))
            gather(1, 0, range(1))
            gather(0, 0, range(2, 3))
            gather(1, 0, range(1, 3))
            project(last)
            gather(0, 1, range(G), low)
            gather(1, 1, range(G), low)
            gather(0, 1, range(G, GROUPS), low)
            gather(1, 1, range(G, GROUPS), low)
            gather(0, 1, range(GROUPS), high)
            gather(1, 1, range(GROUPS), high)
            empty_y(last - 1)
            store_y(last - 1, 1)
            store_c(nc.scalar.copy, 0, 0)
            store_c(nc.scalar.copy, 1, 0)
            empty_y(last)
            store_y(last, 1)
            store_c(nc.vector.tensor_copy, 0, 1, low)
            store_c(nc.scalar.copy, 1, 1, low)
            store_c(nc.vector.tensor_copy, 0, 1, high)
            store_c(nc.scalar.copy, 1, 1, high)
